import numpy as np
import ml_dtypes


def mxq(x, axis, fmt="e4m3"):
    dtype, down = {"e4m3": (ml_dtypes.float8_e4m3fn, 7), "e5m2": (ml_dtypes.float8_e5m2, 14)}[fmt]
    v = np.moveaxis(np.asarray(x, np.float32).astype(ml_dtypes.bfloat16).astype(np.float64), axis, -1)
    blocks = v.reshape(v.shape[:-1] + (-1, 32))
    amax = np.abs(blocks).max(-1, keepdims=True)
    byte = np.maximum(np.where(amax > 0, np.frexp(amax)[1] - 1 + 127, 0) - down, 1)
    scale = np.exp2(byte - 127.0)
    codes = (blocks / scale).astype(np.float32).astype(dtype).astype(np.float64)
    return np.moveaxis((codes * scale).reshape(v.shape), -1, axis)


WIDE = False


def mx_kscale(k):
    if not WIDE:
        return np.ones(k)
    levels = np.array([10, -10, 5, -5, 0])
    if k % 512:
        return np.exp2(np.random.permutation(np.resize(levels, k // 32))).repeat(32)
    a = np.empty((k // 512, 16))
    for p in range(k // 512):
        a[p, :8] = np.random.permutation(np.resize(levels, 8))
        for g in range(8):
            far = levels[np.abs(levels - a[p, g]) >= 10]
            a[p, g + 8] = far[np.random.randint(len(far))]
    return np.exp2(a.ravel()).repeat(32)


def f64(x):
    return np.asarray(x).astype(np.float64)


def striped(idx):
    return np.tile(idx.reshape(-1, 16).T, (8, 1)).astype(np.uint16)


def unstriped(offs):
    return offs[:16].T.reshape(-1).astype(np.int64)


E2M1 = np.array([0.0, 0.5, 1.0, 1.5, 2.0, 3.0, 4.0, 6.0, -0.0, -0.5, -1.0, -1.5, -2.0, -3.0, -4.0, -6.0])


def pack_weight(w, fmt):
    k, n = w.shape
    w = f64(np.asarray(w, np.float32).astype(ml_dtypes.bfloat16)).reshape(k // 32, 32, n)
    amax = np.abs(w).max(1)
    if fmt == "e4m3":
        byte = np.frexp(amax)[1] - 1 + 127 - 7
    else:
        mant, ex = np.frexp(amax / 6.0)
        byte = np.where(mant > 0.5, ex, ex - 1) + 127
    byte = np.clip(np.where(amax > 0, byte, 1), 1, 254)
    scaled = (w * np.exp2(127.0 - byte)[:, None, :]).reshape(k, n).astype(np.float32)
    by_word = np.ascontiguousarray(scaled.reshape(k // 512, 128, 4, n).transpose(0, 1, 3, 2))
    if fmt == "e4m3":
        words = by_word.astype(ml_dtypes.float8_e4m3fn).view(np.uint8)
    else:
        c = by_word.astype(ml_dtypes.float4_e2m1fn).view(np.uint8) & 0xF
        words = (c[..., 0::2] | (c[..., 1::2] << 4)).reshape(k // 512, 128, 2 * n)
    return np.ascontiguousarray(words), np.ascontiguousarray(byte.astype(np.uint8).reshape(k // 512, 16, n))


def unpack_weight(words, scales, fmt):
    g, _, n = scales.shape
    words = np.ascontiguousarray(words).reshape(g, 128, n, -1)
    if fmt == "e4m3":
        vals = words.view(ml_dtypes.float8_e4m3fn).astype(np.float64)
    else:
        nib = np.empty((g, 128, n, 4), np.uint8)
        nib[..., 0::2] = words & 0xF
        nib[..., 1::2] = words >> 4
        vals = E2M1[nib]
    vals = vals * np.repeat(np.exp2(scales.astype(np.float64) - 127.0), 8, axis=1)[..., None]
    return vals.transpose(0, 1, 3, 2).reshape(g * 512, n)


def relu(v):
    return np.maximum(v, 0.0)


K, T, E, C, H, N = 1024, 512, 4, 256, 512, 128


def by_expert(wq, xq):
    return np.concatenate([wq[e].T @ xq[:, e * C:(e + 1) * C] for e in range(E)], axis=1)


def setup_inputs():
    n = np.random.standard_normal
    s = mx_kscale(K)
    u = mx_kscale(H)
    first = np.random.permutation(np.repeat(np.arange(E), T // E))
    second = (first + 1 + np.random.permutation(np.repeat(np.arange(E - 1), -(-T // (E - 1)))[:T])) % E
    while np.bincount(second, minlength=E).max() != T // E:
        load = np.bincount(second, minlength=E); hi, lo = int(load.argmax()), int(load.argmin())
        t = np.flatnonzero((second == hi) & (first != lo))[0]; second[t] = lo
    slot_token = np.empty(E * C, np.int64); pos = np.empty((2, T), np.int64); fill = np.zeros(E, np.int64)
    place = np.stack([np.random.permutation(C) for _ in range(E)])
    for r, deal in enumerate((first, second)):
        for t in np.random.permutation(T):
            e = deal[t]; j = e * C + place[e, fill[e]]; fill[e] += 1; slot_token[j] = t; pos[r, t] = j
    g = np.random.uniform(0.2, 0.8, T)
    x = pack_weight(n((K, T)) * s[:, None], "e4m3")
    w1 = [pack_weight(m, "e4m3") for m in n((E, K, H)) / np.sqrt(K) / s[None, :, None] * u]
    return {
        "x_words": x[0],
        "x_scales": x[1],
        "w1_words": np.stack([m[0] for m in w1]),
        "w1_scales": np.stack([m[1] for m in w1]),
        "w2": (n((H, N)) / np.sqrt(H) / u[:, None]).astype(np.float32),
        "gate": np.stack([np.tile(g, (128, 1)), np.tile(1.0 - g, (128, 1))]).astype(np.float32),
        "offs": striped(slot_token),
        "pos1": striped(pos[0]),
        "pos2": striped(pos[1]),
    }


def reference(x_words, x_scales, w1_words, w1_scales, w2, gate, offs, pos1, pos2):
    w1 = np.stack([unpack_weight(w1_words[e], w1_scales[e], "e4m3") for e in range(E)])
    w2q = mxq(f64(w2), 0, "e4m3")
    idx = unstriped(offs)
    xq = unpack_weight(x_words, x_scales, "e4m3")[:, idx]
    h = relu(by_expert(w1, xq))
    c = sum(f64(gate[r, :1]) * h[:, unstriped(p)] for r, p in enumerate((pos1, pos2)))
    return w2q.T @ mxq(c, 0, "e4m3")

@@ -1,0 +1,197 @@
+from contextlib import ExitStack
+
+import concourse.mybir as mybir
+from concourse.masks import make_identity
+
+K, T, E, C, H, N = 1024, 512, 4, 256, 512, 128
+S = E * C
+FLOPS = 2 * K * H * S + 2 * H * N * T
+
+F32 = mybir.dt.float32
+BF16 = mybir.dt.bfloat16
+I32 = mybir.dt.int32
+U32 = mybir.dt.uint32
+U16 = mybir.dt.uint16
+U8 = mybir.dt.uint8
+FP8X4 = mybir.dt.float8_e4m3fn_x4
+RELU = mybir.ActivationFunctionType.Relu
+MULT = mybir.AluOpType.mult
+
+P = 128
+PASSES = K // 512
+CHUNKS = H // P
+BANK = 512
+X_LEVEL = 8
+GROUPS = ((0, 256), (256, 128), (384, 128))
+
+
+def tile_moe_sdn_lin_relu_kernel(
+    tc, x_words, x_scales, w1_words, w1_scales, w2, gate, offs, pos1, pos2, out
+):
+    nc = tc.nc
+    with ExitStack() as ctx:
+        lists = ctx.enter_context(tc.tile_pool(name="lists", bufs=1))
+        keep = ctx.enter_context(tc.tile_pool(name="keep", bufs=1))
+        psum = ctx.enter_context(tc.psum_pool(name="psum", bufs=8))
+
+        def bank():
+            return psum.tile([P, BANK], F32, name="bank")
+
+        offs_sb = lists.tile([P, S // 16], U16, name="offs_sb")
+        pos_sb = [lists.tile([P, T // 16], U16, name=f"pos_sb{r}") for r in range(2)]
+
+        xs = keep.tile([P, T], U8, name="xs", align_bytes=64)
+        ws = keep.tile([P, 2, H], U8, name="ws", align_bytes=64)
+        xw = [keep.tile([P, T], I32, name=f"xw{s}", align_bytes=64) for s in range(PASSES)]
+        ww = [keep.tile([P, PASSES, H], I32, name=f"ww{e}", align_bytes=64) for e in range(E)]
+        gate_sb = keep.tile([P, 2, T], F32, name="gate_sb", align_bytes=64)
+        w2_raw = keep.tile([P, 4, N], F32, name="w2_raw", align_bytes=64)
+
+        nc.vector.memset(xs[:].bitcast(I32), 0)
+        nc.vector.memset(ws[:].rearrange("p a i -> p (a i)").bitcast(I32), 0)
+
+        def load_w1_scales(queue, half):
+            for q in range(4):
+                src = w1_scales[2 * half : 2 * half + 2, :, 4 * q : 4 * q + 4, :]
+                queue.dma_start(
+                    ws[32 * q : 32 * q + 16, half, :].bitcast(I32),
+                    src.rearrange("e s b i -> (e s) b i").bitcast(I32),
+                )
+
+        def load_w1_words(e):
+            nc.sync.dma_start(ww[e][:], w1_words[e].rearrange("s p i d -> p s (i d)").bitcast(I32))
+
+        nc.sync.dma_start(offs_sb[:], offs)
+        for q in range(4):
+            nc.scalar.dma_start(
+                xs[32 * q + X_LEVEL : 32 * q + X_LEVEL + 8, :].bitcast(I32),
+                x_scales[:, 4 * q : 4 * q + 4, :].bitcast(I32),
+            )
+        for s in range(PASSES):
+            nc.sync.dma_start(xw[s][:], x_words[s].rearrange("p t d -> p (t d)").bitcast(I32))
+        load_w1_words(0)
+        load_w1_scales(nc.scalar, 0)
+        load_w1_words(1)
+        load_w1_scales(nc.sync, 1)
+        load_w1_words(2)
+        load_w1_words(3)
+        nc.sync.dma_start(pos_sb[0][:], pos1)
+        nc.sync.dma_start(pos_sb[1][:], pos2)
+        nc.sync.dma_start(gate_sb[:], gate.rearrange("r p t -> p r t"))
+        nc.sync.dma_start(w2_raw[:], w2.rearrange("(p j) n -> p j n", j=4))
+
+        ident_raw = keep.tile([P, P], F32, name="ident_raw")
+        ident = keep.tile([P, P], F32, name="ident")
+        make_identity(nc, ident_raw[:])
+        nc.scalar.activation(ident[:], ident_raw[:], RELU)
+
+        h = [keep.tile([P, S], F32, name=f"h{a}", align_bytes=64) for a in range(CHUNKS)]
+        for e in range(E):
+            slots = offs_sb[:, e * C // 16 : (e + 1) * C // 16]
+            gs = keep.tile([P, C], U8, name=f"gs{e}", align_bytes=64)
+            nc.vector.tensor_copy(gs[:], xs[:].indirect(slots))
+            acc = [bank() for a in range(CHUNKS)]
+            for s in range(PASSES):
+                gw = keep.tile([P, C], U32, name=f"gw{e}_{s}", align_bytes=64)
+                nc.vector.tensor_copy(gw[:], xw[s][:].bitcast(U32).indirect(slots))
+                w_level = 4 * (2 * (e % 2) + s)
+                for a in range(CHUNKS):
+                    cols = slice(a * P, (a + 1) * P)
+                    nc.tensor.matmul_mx(
+                        out=acc[a][:, :C],
+                        lhsT=ww[e][:, s, cols].bitcast(FP8X4),
+                        lhsT_scale=ws[w_level:P, e // 2, cols],
+                        rhs=gw[:].bitcast(FP8X4),
+                        rhs_scale=gs[X_LEVEL + 4 * s : P, :],
+                        start=(s == 0),
+                        stop=(s == PASSES - 1),
+                    )
+                    if s == PASSES - 1:
+                        nc.scalar.activation(h[a][:, e * C : (e + 1) * C], acc[a][:, :C], RELU)
+
+        w2_bf = keep.tile([P, N, 4], BF16, name="w2_bf", align_bytes=64)
+        w2_codes = keep.tile([P, N], U32, name="w2_codes", align_bytes=64)
+        w2_scales = keep.tile([P, N], U8, name="w2_scales", align_bytes=64)
+        nc.scalar.copy(w2_bf[:], w2_raw[:].rearrange("p j n -> p n j"))
+        nc.vector.quantize_mx(
+            out=w2_codes[:].bitcast(FP8X4), scales=w2_scales[:], in_=w2_bf[:].rearrange("p n j -> p (n j)")
+        )
+
+        def combine(g):
+            t0, width = GROUPS[g]
+            blocks = width // P
+            ct = [keep.tile([P, 2, P, 2], BF16, name=f"ct{g}_{b}", align_bytes=64) for b in range(blocks)]
+            sums = {}
+            for a in range(CHUNKS):
+                prods = []
+                for r in range(2):
+                    prod = keep.tile([P, width], F32, name=f"prod{g}_{a}_{r}", align_bytes=64)
+                    nc.vector.tensor_tensor(
+                        prod[:],
+                        h[a][:].indirect(pos_sb[r][:, t0 // 16 : (t0 + width) // 16]),
+                        gate_sb[:, r, t0 : t0 + width],
+                        MULT,
+                    )
+                    prods.append(prod)
+                first = 0 if a < CHUNKS - 1 else a
+                for b in range(blocks):
+                    if a == first:
+                        sums[b] = bank()
+                    for r in range(2):
+                        nc.tensor.matmul(
+                            sums[b][:, (a - first) * P : (a - first + 1) * P],
+                            lhsT=prods[r][:, b * P : (b + 1) * P],
+                            rhs=ident[:],
+                            start=(r == 0),
+                            stop=(r == 1),
+                            is_transpose=True,
+                        )
+                    if a >= CHUNKS - 2:
+                        n = a - first + 1
+                        nc.scalar.copy(
+                            ct[b][:, :, 32 * first : 32 * (a + 1), :],
+                            sums[b][:, : n * P].rearrange("t (p u e) -> t u p e", u=2, e=2),
+                        )
+            back = bank()
+            for b in range(blocks):
+                words = ct[b][:].rearrange("t u p e -> t (u p e)").bitcast(F32)
+                for u in range(2):
+                    nc.tensor.transpose(
+                        back[:, u * width + b * P : u * width + (b + 1) * P], words[:, u * P : (u + 1) * P], ident[:]
+                    )
+            c_bf = keep.tile([P, width * 4], BF16, name=f"c_bf{g}", align_bytes=64)
+            nc.scalar.copy(
+                c_bf[:].bitcast(F32).rearrange("p (t u) -> p t u", u=2),
+                back[:, : 2 * width].rearrange("p (u t) -> p t u", u=2),
+            )
+            return c_bf
+
+        def project(g, c_bf):
+            t0, width = GROUPS[g]
+            codes = keep.tile([P, width], U32, name=f"c_codes{g}", align_bytes=64)
+            scales = keep.tile([P, width], U8, name=f"c_scales{g}", align_bytes=64)
+            nc.vector.quantize_mx(out=codes[:].bitcast(FP8X4), scales=scales[:], in_=c_bf[:])
+            acc = bank()
+            nc.tensor.matmul_mx(
+                out=acc[:, :width],
+                lhsT=w2_codes[:].bitcast(FP8X4),
+                lhsT_scale=w2_scales[:],
+                rhs=codes[:].bitcast(FP8X4),
+                rhs_scale=scales[:],
+                start=True,
+                stop=True,
+            )
+            res = keep.tile([P, width], F32, name=f"res{g}", align_bytes=64)
+            if g == 0:
+                nc.scalar.copy(res[:], acc[:, :width])
+            else:
+                nc.vector.tensor_copy(res[:], acc[:, :width])
+            nc.sync.dma_start(out[:, t0 : t0 + width], res[:])
+
+        pending = None
+        for g in range(len(GROUPS)):
+            c_bf = combine(g)
+            if pending is not None:
+                project(*pending)
+            pending = (g, c_bf)
+        project(*pending)

@@ -41,43 +41,38 @@ def tile_moe_sdn_lin_relu_kernel(
         pos_sb = [lists.tile([P, T // 16], U16, name=f"pos_sb{r}") for r in range(2)]
 
         xs = keep.tile([P, T], U8, name="xs", align_bytes=64)
-        ws = keep.tile([P, 2, H], U8, name="ws", align_bytes=64)
+        ws = [keep.tile([P, H], U8, name=f"ws{a}", align_bytes=64) for a in range(2)]
         xw = [keep.tile([P, T], I32, name=f"xw{s}", align_bytes=64) for s in range(PASSES)]
         ww = [keep.tile([P, PASSES, H], I32, name=f"ww{e}", align_bytes=64) for e in range(E)]
         gate_sb = keep.tile([P, 2, T], F32, name="gate_sb", align_bytes=64)
         w2_raw = keep.tile([P, 4, N], F32, name="w2_raw", align_bytes=64)
 
-        nc.vector.memset(xs[:].bitcast(I32), 0)
-        nc.vector.memset(ws[:].rearrange("p a i -> p (a i)").bitcast(I32), 0)
+        nc.gpsimd.memset(xs[:].bitcast(I32), 0)
+        nc.vector.memset(ws[1][:].bitcast(I32), 0)
 
-        def load_w1_scales(queue, half):
-            for q in range(4):
-                src = w1_scales[2 * half : 2 * half + 2, :, 4 * q : 4 * q + 4, :]
-                queue.dma_start(
-                    ws[32 * q : 32 * q + 16, half, :].bitcast(I32),
-                    src.rearrange("e s b i -> (e s) b i").bitcast(I32),
-                )
+        def load_w1_words(queue, e):
+            queue.dma_start(ww[e][:], w1_words[e].rearrange("s p i d -> p s (i d)").bitcast(I32))
 
-        def load_w1_words(e):
-            nc.sync.dma_start(ww[e][:], w1_words[e].rearrange("s p i d -> p s (i d)").bitcast(I32))
-
+        planes = w1_scales.rearrange("e s b i -> (e s) b i").bitcast(I32)
         nc.sync.dma_start(offs_sb[:], offs)
         for q in range(4):
-            nc.scalar.dma_start(
+            (nc.sync if q < 2 else nc.scalar).dma_start(
                 xs[32 * q + X_LEVEL : 32 * q + X_LEVEL + 8, :].bitcast(I32),
                 x_scales[:, 4 * q : 4 * q + 4, :].bitcast(I32),
             )
-        for s in range(PASSES):
-            nc.sync.dma_start(xw[s][:], x_words[s].rearrange("p t d -> p (t d)").bitcast(I32))
-        load_w1_words(0)
-        load_w1_scales(nc.scalar, 0)
-        load_w1_words(1)
-        load_w1_scales(nc.sync, 1)
-        load_w1_words(2)
-        load_w1_words(3)
+        for s, queue in enumerate((nc.sync, nc.scalar)):
+            queue.dma_start(xw[s][:], x_words[s].rearrange("p t d -> p (t d)").bitcast(I32))
+        load_w1_words(nc.sync, 0)
+        for q in range(4):
+            nc.scalar.dma_start(ws[0][32 * q : 32 * q + 32, :].bitcast(I32), planes[:, 4 * q : 4 * q + 4, :])
+        load_w1_words(nc.sync, 1)
+        load_w1_words(nc.sync, 2)
+        for q in range(4):
+            nc.sync.dma_start(ws[1][32 * q : 32 * q + 16, :].bitcast(I32), planes[4:8, 4 * q : 4 * q + 4, :])
+        load_w1_words(nc.sync, 3)
+        nc.sync.dma_start(gate_sb[:], gate.rearrange("r p t -> p r t"))
         nc.sync.dma_start(pos_sb[0][:], pos1)
         nc.sync.dma_start(pos_sb[1][:], pos2)
-        nc.sync.dma_start(gate_sb[:], gate.rearrange("r p t -> p r t"))
         nc.sync.dma_start(w2_raw[:], w2.rearrange("(p j) n -> p j n", j=4))
 
         ident_raw = keep.tile([P, P], F32, name="ident_raw")
@@ -100,7 +95,7 @@ def tile_moe_sdn_lin_relu_kernel(
                     nc.tensor.matmul_mx(
                         out=acc[a][:, :C],
                         lhsT=ww[e][:, s, cols].bitcast(FP8X4),
-                        lhsT_scale=ws[w_level:P, e // 2, cols],
+                        lhsT_scale=ws[e // 2][w_level:P, cols],
                         rhs=gw[:].bitcast(FP8X4),
                         rhs_scale=gs[X_LEVEL + 4 * s : P, :],
                         start=(s == 0),
@@ -182,16 +177,9 @@ def tile_moe_sdn_lin_relu_kernel(
                 stop=True,
             )
             res = keep.tile([P, width], F32, name=f"res{g}", align_bytes=64)
-            if g == 0:
-                nc.scalar.copy(res[:], acc[:, :width])
-            else:
-                nc.vector.tensor_copy(res[:], acc[:, :width])
+            nc.vector.tensor_copy(res[:], acc[:, :width])
             nc.sync.dma_start(out[:, t0 : t0 + width], res[:])
 
-        pending = None
+        rounded = [combine(g) for g in range(len(GROUPS))]
         for g in range(len(GROUPS)):
-            c_bf = combine(g)
-            if pending is not None:
-                project(*pending)
-            pending = (g, c_bf)
-        project(*pending)
+            project(g, rounded[g])

@@ -22,6 +22,7 @@ PASSES = K // 512
 CHUNKS = H // P
 BANK = 512
 X_LEVEL = 8
+GATHERS = ((0, 384), (384, 128))
 GROUPS = ((0, 256), (256, 128), (384, 128))
 
 
@@ -43,7 +44,8 @@ def tile_moe_sdn_lin_relu_kernel(
         xs = keep.tile([P, T], U8, name="xs", align_bytes=64)
         ws = [keep.tile([P, H], U8, name=f"ws{a}", align_bytes=64) for a in range(2)]
         xw = [keep.tile([P, T], I32, name=f"xw{s}", align_bytes=64) for s in range(PASSES)]
-        ww = [keep.tile([P, PASSES, H], I32, name=f"ww{e}", align_bytes=64) for e in range(E)]
+        ww = [keep.tile([P, PASSES, H if e < 2 else H // 2], I32, name=f"ww{e}", align_bytes=64) for e in range(E)]
+        late = keep.tile([P, 2 * PASSES, H // 2], I32, name="late", align_bytes=64)
         gate_sb = keep.tile([P, 2, T], F32, name="gate_sb", align_bytes=64)
         w2_raw = keep.tile([P, 4, N], F32, name="w2_raw", align_bytes=64)
 
@@ -53,27 +55,37 @@ def tile_moe_sdn_lin_relu_kernel(
         def load_w1_words(queue, e):
             queue.dma_start(ww[e][:], w1_words[e].rearrange("s p i d -> p s (i d)").bitcast(I32))
 
+        def load_w1_half(e):
+            nc.sync.dma_start(ww[e][:], w1_words[e, :, :, : H // 2, :].rearrange("s p i d -> p s (i d)").bitcast(I32))
+
         planes = w1_scales.rearrange("e s b i -> (e s) b i").bitcast(I32)
-        nc.sync.dma_start(offs_sb[:], offs)
+        def load_first_w1_scales(q):
+            nc.sync.dma_start(ws[0][32 * q : 32 * q + 32, :].bitcast(I32), planes[:, 4 * q : 4 * q + 4, :])
+
+        load_w1_words(nc.gpsimd, 0)
+        for s in range(PASSES):
+            nc.scalar.dma_start(xw[s][:], x_words[s].rearrange("p t d -> p (t d)").bitcast(I32))
+        load_first_w1_scales(0)
         for q in range(4):
-            (nc.sync if q < 2 else nc.scalar).dma_start(
+            nc.sync.dma_start(
                 xs[32 * q + X_LEVEL : 32 * q + X_LEVEL + 8, :].bitcast(I32),
                 x_scales[:, 4 * q : 4 * q + 4, :].bitcast(I32),
             )
-        for s, queue in enumerate((nc.sync, nc.scalar)):
-            queue.dma_start(xw[s][:], x_words[s].rearrange("p t d -> p (t d)").bitcast(I32))
-        load_w1_words(nc.sync, 0)
-        for q in range(4):
-            nc.scalar.dma_start(ws[0][32 * q : 32 * q + 32, :].bitcast(I32), planes[:, 4 * q : 4 * q + 4, :])
+        nc.sync.dma_start(offs_sb[:], offs)
+        for q in range(1, 4):
+            load_first_w1_scales(q)
         load_w1_words(nc.sync, 1)
-        load_w1_words(nc.sync, 2)
+        load_w1_half(2)
         for q in range(4):
             nc.sync.dma_start(ws[1][32 * q : 32 * q + 16, :].bitcast(I32), planes[4:8, 4 * q : 4 * q + 4, :])
-        load_w1_words(nc.sync, 3)
+        nc.sync.dma_start(w2_raw[:], w2.rearrange("(p j) n -> p j n", j=4))
+        load_w1_half(3)
+        nc.sync.dma_start(
+            late[:], w1_words[2:4, :, :, H // 2 :, :].rearrange("e s p i d -> p (e s) (i d)").bitcast(I32)
+        )
         nc.sync.dma_start(gate_sb[:], gate.rearrange("r p t -> p r t"))
         nc.sync.dma_start(pos_sb[0][:], pos1)
         nc.sync.dma_start(pos_sb[1][:], pos2)
-        nc.sync.dma_start(w2_raw[:], w2.rearrange("(p j) n -> p j n", j=4))
 
         ident_raw = keep.tile([P, P], F32, name="ident_raw")
         ident = keep.tile([P, P], F32, name="ident")
@@ -81,28 +93,47 @@ def tile_moe_sdn_lin_relu_kernel(
         nc.scalar.activation(ident[:], ident_raw[:], RELU)
 
         h = [keep.tile([P, S], F32, name=f"h{a}", align_bytes=64) for a in range(CHUNKS)]
+        gs = [keep.tile([P, C], U8, name=f"gs{e}", align_bytes=64) for e in range(E)]
+        gw = [[keep.tile([P, C], U32, name=f"gw{e}_{s}", align_bytes=64) for s in range(PASSES)] for e in range(E)]
+
+        def hidden(e, steps):
+            acc = {}
+            for a, s, lo, hi in steps:
+                if s == 0:
+                    acc[a, lo] = bank()
+                if e < 2 or a < 2:
+                    words = ww[e][:, s, a * P : (a + 1) * P]
+                else:
+                    words = late[:, PASSES * (e - 2) + s, (a - 2) * P : (a - 1) * P]
+                nc.tensor.matmul_mx(
+                    out=acc[a, lo][:, : hi - lo],
+                    lhsT=words.bitcast(FP8X4),
+                    lhsT_scale=ws[e // 2][4 * (2 * (e % 2) + s) : P, a * P : (a + 1) * P],
+                    rhs=gw[e][s][:, lo:hi].bitcast(FP8X4),
+                    rhs_scale=gs[e][X_LEVEL + 4 * s : P, lo:hi],
+                    start=(s == 0),
+                    stop=(s == PASSES - 1),
+                )
+                if s == PASSES - 1:
+                    nc.scalar.activation(h[a][:, e * C + lo : e * C + hi], acc[a, lo][:, : hi - lo], RELU)
+
         for e in range(E):
             slots = offs_sb[:, e * C // 16 : (e + 1) * C // 16]
-            gs = keep.tile([P, C], U8, name=f"gs{e}", align_bytes=64)
-            nc.vector.tensor_copy(gs[:], xs[:].indirect(slots))
-            acc = [bank() for a in range(CHUNKS)]
+            nc.vector.tensor_copy(gs[e][:], xs[:].indirect(slots))
             for s in range(PASSES):
-                gw = keep.tile([P, C], U32, name=f"gw{e}_{s}", align_bytes=64)
-                nc.vector.tensor_copy(gw[:], xw[s][:].bitcast(U32).indirect(slots))
-                w_level = 4 * (2 * (e % 2) + s)
-                for a in range(CHUNKS):
-                    cols = slice(a * P, (a + 1) * P)
-                    nc.tensor.matmul_mx(
-                        out=acc[a][:, :C],
-                        lhsT=ww[e][:, s, cols].bitcast(FP8X4),
-                        lhsT_scale=ws[e // 2][w_level:P, cols],
-                        rhs=gw[:].bitcast(FP8X4),
-                        rhs_scale=gs[X_LEVEL + 4 * s : P, :],
-                        start=(s == 0),
-                        stop=(s == PASSES - 1),
-                    )
-                    if s == PASSES - 1:
-                        nc.scalar.activation(h[a][:, e * C : (e + 1) * C], acc[a][:, :C], RELU)
+                pieces = 2 if (e, s) == (E - 1, PASSES - 1) else 1
+                for i in range(pieces):
+                    lo, hi = i * C // pieces, (i + 1) * C // pieces
+                    part = offs_sb[:, (e * C + lo) // 16 : (e * C + hi) // 16]
+                    nc.vector.tensor_copy(gw[e][s][:, lo:hi], xw[s][:].bitcast(U32).indirect(part))
+            chunks = range(CHUNKS if e < 2 else 2)
+            if e < E - 1:
+                hidden(e, [(a, s, 0, C) for a in chunks for s in range(PASSES)])
+            else:
+                hidden(e, [(a, s, lo, lo + P) for s in range(PASSES) for lo in (0, P) for a in chunks])
+        for a in range(2, CHUNKS):
+            for e in range(2, E):
+                hidden(e, [(a, s, 0, C) for s in range(PASSES)])
 
         w2_bf = keep.tile([P, N, 4], BF16, name="w2_bf", align_bytes=64)
         w2_codes = keep.tile([P, N], U32, name="w2_codes", align_bytes=64)
@@ -112,15 +143,14 @@ def tile_moe_sdn_lin_relu_kernel(
             out=w2_codes[:].bitcast(FP8X4), scales=w2_scales[:], in_=w2_bf[:].rearrange("p n j -> p (n j)")
         )
 
-        def combine(g):
-            t0, width = GROUPS[g]
-            blocks = width // P
-            ct = [keep.tile([P, 2, P, 2], BF16, name=f"ct{g}_{b}", align_bytes=64) for b in range(blocks)]
+        ct = [keep.tile([P, 2, P, 2], BF16, name=f"ct{b}", align_bytes=64) for b in range(T // P)]
+
+        def combine(t0, width):
             sums = {}
             for a in range(CHUNKS):
                 prods = []
                 for r in range(2):
-                    prod = keep.tile([P, width], F32, name=f"prod{g}_{a}_{r}", align_bytes=64)
+                    prod = keep.tile([P, width], F32, name=f"prod{t0}_{a}_{r}", align_bytes=64)
                     nc.vector.tensor_tensor(
                         prod[:],
                         h[a][:].indirect(pos_sb[r][:, t0 // 16 : (t0 + width) // 16]),
@@ -129,7 +159,7 @@ def tile_moe_sdn_lin_relu_kernel(
                     )
                     prods.append(prod)
                 first = 0 if a < CHUNKS - 1 else a
-                for b in range(blocks):
+                for b in range(width // P):
                     if a == first:
                         sums[b] = bank()
                     for r in range(2):
@@ -144,12 +174,15 @@ def tile_moe_sdn_lin_relu_kernel(
                     if a >= CHUNKS - 2:
                         n = a - first + 1
                         nc.scalar.copy(
-                            ct[b][:, :, 32 * first : 32 * (a + 1), :],
+                            ct[t0 // P + b][:, :, 32 * first : 32 * (a + 1), :],
                             sums[b][:, : n * P].rearrange("t (p u e) -> t u p e", u=2, e=2),
                         )
+
+        def turn_back(g):
+            t0, width = GROUPS[g]
             back = bank()
-            for b in range(blocks):
-                words = ct[b][:].rearrange("t u p e -> t (u p e)").bitcast(F32)
+            for b in range(width // P):
+                words = ct[t0 // P + b][:].rearrange("t u p e -> t (u p e)").bitcast(F32)
                 for u in range(2):
                     nc.tensor.transpose(
                         back[:, u * width + b * P : u * width + (b + 1) * P], words[:, u * P : (u + 1) * P], ident[:]
@@ -180,6 +213,9 @@ def tile_moe_sdn_lin_relu_kernel(
             nc.vector.tensor_copy(res[:], acc[:, :width])
             nc.sync.dma_start(out[:, t0 : t0 + width], res[:])
 
-        rounded = [combine(g) for g in range(len(GROUPS))]
+        rounded = []
+        for t0, width in GATHERS:
+            combine(t0, width)
+            rounded.extend(turn_back(g) for g in range(len(GROUPS)) if t0 <= GROUPS[g][0] < t0 + width)
         for g in range(len(GROUPS)):
             project(g, rounded[g])

@@ -22,6 +22,8 @@ PASSES = K // 512
 CHUNKS = H // P
 BANK = 512
 X_LEVEL = 8
+WORD_WINDOW = (1408, 704)
+BYTE_WINDOW = 704
 GATHERS = ((0, 384), (384, 128))
 GROUPS = ((0, 256), (256, 128), (384, 128))
 
@@ -41,51 +43,45 @@ def tile_moe_sdn_lin_relu_kernel(
         offs_sb = lists.tile([P, S // 16], U16, name="offs_sb")
         pos_sb = [lists.tile([P, T // 16], U16, name=f"pos_sb{r}") for r in range(2)]
 
-        xs = keep.tile([P, T], U8, name="xs", align_bytes=64)
-        ws = [keep.tile([P, H], U8, name=f"ws{a}", align_bytes=64) for a in range(2)]
-        xw = [keep.tile([P, T], I32, name=f"xw{s}", align_bytes=64) for s in range(PASSES)]
-        ww = [keep.tile([P, PASSES, H if e < 2 else H // 2], I32, name=f"ww{e}", align_bytes=64) for e in range(E)]
-        late = keep.tile([P, 2 * PASSES, H // 2], I32, name="late", align_bytes=64)
+        xs = keep.tile([P, BYTE_WINDOW], U8, name="xs", align_bytes=64)
+        ws = keep.tile([P, E * PASSES * H], U8, name="ws", align_bytes=64)
+        xw = [keep.tile([P, WORD_WINDOW[s]], I32, name=f"xw{s}", align_bytes=64) for s in range(PASSES)]
+        ww = [keep.tile([P, E * PASSES, H // 2], I32, name=f"ww{half}", align_bytes=64) for half in range(2)]
         gate_sb = keep.tile([P, 2, T], F32, name="gate_sb", align_bytes=64)
         w2_raw = keep.tile([P, 4, N], F32, name="w2_raw", align_bytes=64)
 
         nc.gpsimd.memset(xs[:].bitcast(I32), 0)
-        nc.vector.memset(ws[1][:].bitcast(I32), 0)
-
-        def load_w1_words(queue, e):
-            queue.dma_start(ww[e][:], w1_words[e].rearrange("s p i d -> p s (i d)").bitcast(I32))
-
-        def load_w1_half(e):
-            nc.sync.dma_start(ww[e][:], w1_words[e, :, :, : H // 2, :].rearrange("s p i d -> p s (i d)").bitcast(I32))
-
-        planes = w1_scales.rearrange("e s b i -> (e s) b i").bitcast(I32)
-        def load_first_w1_scales(q):
-            nc.sync.dma_start(ws[0][32 * q : 32 * q + 32, :].bitcast(I32), planes[:, 4 * q : 4 * q + 4, :])
-
-        load_w1_words(nc.gpsimd, 0)
         for s in range(PASSES):
-            nc.scalar.dma_start(xw[s][:], x_words[s].rearrange("p t d -> p (t d)").bitcast(I32))
-        load_first_w1_scales(0)
+            nc.vector.memset(xw[s][:, T:], 0)
+        nc.vector.memset(ws[:].bitcast(I32), 0)
+
+        def load_w1_half(half):
+            cols = slice(half * H // 2, (half + 1) * H // 2)
+            nc.sync.dma_start(
+                ww[half][:], w1_words[:, :, :, cols, :].rearrange("e s p i d -> p (e s) (i d)").bitcast(I32)
+            )
+
+        rows = w1_scales.rearrange("e s (q r) i -> r q (e s) i", r=4).bitcast(I32)
+
+        def load_x_words(s):
+            nc.sync.dma_start(xw[s][:, :T], x_words[s].rearrange("p t d -> p (t d)").bitcast(I32))
+
+        nc.sync.dma_start(offs_sb[:], offs)
+        load_x_words(0)
         for q in range(4):
             nc.sync.dma_start(
-                xs[32 * q + X_LEVEL : 32 * q + X_LEVEL + 8, :].bitcast(I32),
+                xs[32 * q + X_LEVEL : 32 * q + X_LEVEL + 8, :T].bitcast(I32),
                 x_scales[:, 4 * q : 4 * q + 4, :].bitcast(I32),
             )
-        nc.sync.dma_start(offs_sb[:], offs)
-        for q in range(1, 4):
-            load_first_w1_scales(q)
-        load_w1_words(nc.sync, 1)
-        load_w1_half(2)
-        for q in range(4):
-            nc.sync.dma_start(ws[1][32 * q : 32 * q + 16, :].bitcast(I32), planes[4:8, 4 * q : 4 * q + 4, :])
-        nc.sync.dma_start(w2_raw[:], w2.rearrange("(p j) n -> p j n", j=4))
-        load_w1_half(3)
-        nc.sync.dma_start(
-            late[:], w1_words[2:4, :, :, H // 2 :, :].rearrange("e s p i d -> p (e s) (i d)").bitcast(I32)
-        )
+        load_x_words(1)
+        load_w1_half(0)
+        for r in range(4):
+            nc.sync.dma_start(ws[r:P:32, :].bitcast(I32).rearrange("q (g i) -> q g i", g=E * PASSES), rows[r])
+        load_w1_half(1)
         nc.sync.dma_start(gate_sb[:], gate.rearrange("r p t -> p r t"))
         nc.sync.dma_start(pos_sb[0][:], pos1)
         nc.sync.dma_start(pos_sb[1][:], pos2)
+        nc.sync.dma_start(w2_raw[:], w2.rearrange("(p j) n -> p j n", j=4))
 
         ident_raw = keep.tile([P, P], F32, name="ident_raw")
         ident = keep.tile([P, P], F32, name="ident")
@@ -93,47 +89,46 @@ def tile_moe_sdn_lin_relu_kernel(
         nc.scalar.activation(ident[:], ident_raw[:], RELU)
 
         h = [keep.tile([P, S], F32, name=f"h{a}", align_bytes=64) for a in range(CHUNKS)]
-        gs = [keep.tile([P, C], U8, name=f"gs{e}", align_bytes=64) for e in range(E)]
-        gw = [[keep.tile([P, C], U32, name=f"gw{e}_{s}", align_bytes=64) for s in range(PASSES)] for e in range(E)]
+        gs = keep.tile([P, S], U8, name="gs", align_bytes=64)
+        gw = [keep.tile([P, S], U32, name=f"gw{s}", align_bytes=64) for s in range(PASSES)]
 
-        def hidden(e, steps):
-            acc = {}
+        def gather_words(s, lo, hi):
+            nc.vector.tensor_copy(gw[s][:, lo:hi], xw[s][:].bitcast(U32).indirect(offs_sb[:, lo // 16 : hi // 16]))
+
+        acc = {}
+
+        def hidden(steps):
             for a, s, lo, hi in steps:
+                e = lo // C
                 if s == 0:
                     acc[a, lo] = bank()
-                if e < 2 or a < 2:
-                    words = ww[e][:, s, a * P : (a + 1) * P]
-                else:
-                    words = late[:, PASSES * (e - 2) + s, (a - 2) * P : (a - 1) * P]
                 nc.tensor.matmul_mx(
                     out=acc[a, lo][:, : hi - lo],
-                    lhsT=words.bitcast(FP8X4),
-                    lhsT_scale=ws[e // 2][4 * (2 * (e % 2) + s) : P, a * P : (a + 1) * P],
-                    rhs=gw[e][s][:, lo:hi].bitcast(FP8X4),
-                    rhs_scale=gs[e][X_LEVEL + 4 * s : P, lo:hi],
+                    lhsT=ww[a // 2][:, PASSES * e + s, (a % 2) * P : (a % 2 + 1) * P].bitcast(FP8X4),
+                    lhsT_scale=ws[:, (PASSES * e + s) * H + a * P : (PASSES * e + s) * H + (a + 1) * P],
+                    rhs=gw[s][:, lo:hi].bitcast(FP8X4),
+                    rhs_scale=gs[X_LEVEL + 4 * s : P, lo:hi],
                     start=(s == 0),
                     stop=(s == PASSES - 1),
                 )
                 if s == PASSES - 1:
-                    nc.scalar.activation(h[a][:, e * C + lo : e * C + hi], acc[a, lo][:, : hi - lo], RELU)
+                    nc.scalar.activation(h[a][:, lo:hi], acc[a, lo][:, : hi - lo], RELU)
 
-        for e in range(E):
-            slots = offs_sb[:, e * C // 16 : (e + 1) * C // 16]
-            nc.vector.tensor_copy(gs[e][:], xs[:].indirect(slots))
-            for s in range(PASSES):
-                pieces = 2 if (e, s) == (E - 1, PASSES - 1) else 1
-                for i in range(pieces):
-                    lo, hi = i * C // pieces, (i + 1) * C // pieces
-                    part = offs_sb[:, (e * C + lo) // 16 : (e * C + hi) // 16]
-                    nc.vector.tensor_copy(gw[e][s][:, lo:hi], xw[s][:].bitcast(U32).indirect(part))
-            chunks = range(CHUNKS if e < 2 else 2)
-            if e < E - 1:
-                hidden(e, [(a, s, 0, C) for a in chunks for s in range(PASSES)])
-            else:
-                hidden(e, [(a, s, lo, lo + P) for s in range(PASSES) for lo in (0, P) for a in chunks])
+        gather_words(0, 0, S)
+        for lo in (0, 2 * C):
+            nc.vector.tensor_copy(gs[:, lo : lo + 2 * C], xs[:].indirect(offs_sb[:, lo // 16 : (lo + 2 * C) // 16]))
+        gather_words(1, 0, 2 * C)
+        gather_words(1, 2 * C, 3 * C)
+        gather_words(1, 3 * C, 3 * C + P)
+        gather_words(1, 3 * C + P, S)
+        whole = [(e * C, (e + 1) * C) for e in range(E)]
+        first = whole[:3] + [(3 * C, 3 * C + P), (3 * C + P, S)]
+        hidden([(a, 0, lo, hi) for a in range(2) for lo, hi in whole[:2]])
+        hidden([(0, 0, lo, hi) for lo, hi in first[2:]] + [(1, 0, *whole[2])])
+        hidden([(0, 1, lo, hi) for lo, hi in first])
+        hidden([(1, 1, lo, hi) for lo, hi in whole[:3]] + [(1, s, *whole[3]) for s in range(PASSES)])
         for a in range(2, CHUNKS):
-            for e in range(2, E):
-                hidden(e, [(a, s, 0, C) for s in range(PASSES)])
+            hidden([(a, s, lo, hi) for lo, hi in whole for s in range(PASSES)])
 
         w2_bf = keep.tile([P, N, 4], BF16, name="w2_bf", align_bytes=64)
         w2_codes = keep.tile([P, N], U32, name="w2_codes", align_bytes=64)
@@ -199,9 +194,9 @@ def tile_moe_sdn_lin_relu_kernel(
             codes = keep.tile([P, width], U32, name=f"c_codes{g}", align_bytes=64)
             scales = keep.tile([P, width], U8, name=f"c_scales{g}", align_bytes=64)
             nc.vector.quantize_mx(out=codes[:].bitcast(FP8X4), scales=scales[:], in_=c_bf[:])
-            acc = bank()
+            proj = bank()
             nc.tensor.matmul_mx(
-                out=acc[:, :width],
+                out=proj[:, :width],
                 lhsT=w2_codes[:].bitcast(FP8X4),
                 lhsT_scale=w2_scales[:],
                 rhs=codes[:].bitcast(FP8X4),
@@ -210,7 +205,7 @@ def tile_moe_sdn_lin_relu_kernel(
                 stop=True,
             )
             res = keep.tile([P, width], F32, name=f"res{g}", align_bytes=64)
-            nc.vector.tensor_copy(res[:], acc[:, :width])
+            nc.vector.tensor_copy(res[:], proj[:, :width])
             nc.sync.dma_start(out[:, t0 : t0 + width], res[:])
 
         rounded = []

@@ -35,10 +35,10 @@ def tile_moe_sdn_lin_relu_kernel(
     with ExitStack() as ctx:
         lists = ctx.enter_context(tc.tile_pool(name="lists", bufs=1))
         keep = ctx.enter_context(tc.tile_pool(name="keep", bufs=1))
-        psum = ctx.enter_context(tc.psum_pool(name="psum", bufs=8))
+        psum = ctx.enter_context(tc.psum_pool(name="psum", bufs=1))
 
-        def bank():
-            return psum.tile([P, BANK], F32, name="bank")
+        def bank(n):
+            return psum.tile([P, BANK], F32, name=f"bank{n}")
 
         offs_sb = lists.tile([P, S // 16], U16, name="offs_sb")
         pos_sb = [lists.tile([P, T // 16], U16, name=f"pos_sb{r}") for r in range(2)]
@@ -46,7 +46,9 @@ def tile_moe_sdn_lin_relu_kernel(
         xs = keep.tile([P, BYTE_WINDOW], U8, name="xs", align_bytes=64)
         ws = keep.tile([P, E * PASSES * H], U8, name="ws", align_bytes=64)
         xw = [keep.tile([P, WORD_WINDOW[s]], I32, name=f"xw{s}", align_bytes=64) for s in range(PASSES)]
-        ww = [keep.tile([P, E * PASSES, H // 2], I32, name=f"ww{half}", align_bytes=64) for half in range(2)]
+        ww_early = [keep.tile([P, 2 * PASSES, H // 2], I32, name=f"ww_early{pair}", align_bytes=64) for pair in range(2)]
+        ww_late = keep.tile([P, E * PASSES, H // 2], I32, name="ww_late", align_bytes=64)
+        gate_row = keep.tile([P, 2, 4], F32, name="gate_row", align_bytes=64)
         gate_sb = keep.tile([P, 2, T], F32, name="gate_sb", align_bytes=64)
         w2_raw = keep.tile([P, 4, N], F32, name="w2_raw", align_bytes=64)
 
@@ -55,10 +57,9 @@ def tile_moe_sdn_lin_relu_kernel(
             nc.vector.memset(xw[s][:, T:], 0)
         nc.vector.memset(ws[:].bitcast(I32), 0)
 
-        def load_w1_half(half):
-            cols = slice(half * H // 2, (half + 1) * H // 2)
+        def load_w1(tile, experts, cols):
             nc.sync.dma_start(
-                ww[half][:], w1_words[:, :, :, cols, :].rearrange("e s p i d -> p (e s) (i d)").bitcast(I32)
+                tile[:], w1_words[experts, :, :, cols, :].rearrange("e s p i d -> p (e s) (i d)").bitcast(I32)
             )
 
         rows = w1_scales.rearrange("e s (q r) i -> r q (e s) i", r=4).bitcast(I32)
@@ -74,19 +75,30 @@ def tile_moe_sdn_lin_relu_kernel(
                 x_scales[:, 4 * q : 4 * q + 4, :].bitcast(I32),
             )
         load_x_words(1)
-        load_w1_half(0)
+        load_w1(ww_early[0], slice(0, 2), slice(0, H // 2))
+        nc.sync.dma_start(gate_row[:], gate[:, 0, :].rearrange("r (n m) -> n r m", m=4))
+        load_w1(ww_early[1], slice(2, 4), slice(0, H // 2))
         for r in range(4):
             nc.sync.dma_start(ws[r:P:32, :].bitcast(I32).rearrange("q (g i) -> q g i", g=E * PASSES), rows[r])
-        load_w1_half(1)
-        nc.sync.dma_start(gate_sb[:], gate.rearrange("r p t -> p r t"))
+        nc.sync.dma_start(w2_raw[:], w2.rearrange("(p j) n -> p j n", j=4))
         nc.sync.dma_start(pos_sb[0][:], pos1)
         nc.sync.dma_start(pos_sb[1][:], pos2)
-        nc.sync.dma_start(w2_raw[:], w2.rearrange("(p j) n -> p j n", j=4))
+        load_w1(ww_late, slice(0, E), slice(H // 2, H))
 
         ident_raw = keep.tile([P, P], F32, name="ident_raw")
         ident = keep.tile([P, P], F32, name="ident")
         make_identity(nc, ident_raw[:])
         nc.scalar.activation(ident[:], ident_raw[:], RELU)
+
+        for r in range(2):
+            spread = bank(6 + r)
+            for m in range(4):
+                nc.tensor.transpose(
+                    spread[:, m * P : (m + 1) * P], gate_row[:, r, m : m + 1].to_broadcast([P, P]), ident[:]
+                )
+            nc.scalar.copy(
+                gate_sb[:, r, :].rearrange("p (n m) -> p n m", m=4), spread[:].rearrange("p (m n) -> p n m", m=4)
+            )
 
         h = [keep.tile([P, S], F32, name=f"h{a}", align_bytes=64) for a in range(CHUNKS)]
         gs = keep.tile([P, S], U8, name="gs", align_bytes=64)
@@ -101,10 +113,11 @@ def tile_moe_sdn_lin_relu_kernel(
             for a, s, lo, hi in steps:
                 e = lo // C
                 if s == 0:
-                    acc[a, lo] = bank()
+                    acc[a, lo] = bank(len(acc) % 8)
+                words = ww_early[e // 2][:, PASSES * (e % 2) + s] if a < 2 else ww_late[:, PASSES * e + s]
                 nc.tensor.matmul_mx(
                     out=acc[a, lo][:, : hi - lo],
-                    lhsT=ww[a // 2][:, PASSES * e + s, (a % 2) * P : (a % 2 + 1) * P].bitcast(FP8X4),
+                    lhsT=words[:, (a % 2) * P : (a % 2 + 1) * P].bitcast(FP8X4),
                     lhsT_scale=ws[:, (PASSES * e + s) * H + a * P : (PASSES * e + s) * H + (a + 1) * P],
                     rhs=gw[s][:, lo:hi].bitcast(FP8X4),
                     rhs_scale=gs[X_LEVEL + 4 * s : P, lo:hi],
@@ -133,21 +146,27 @@ def tile_moe_sdn_lin_relu_kernel(
         w2_bf = keep.tile([P, N, 4], BF16, name="w2_bf", align_bytes=64)
         w2_codes = keep.tile([P, N], U32, name="w2_codes", align_bytes=64)
         w2_scales = keep.tile([P, N], U8, name="w2_scales", align_bytes=64)
-        nc.scalar.copy(w2_bf[:], w2_raw[:].rearrange("p j n -> p n j"))
+        nc.vector.tensor_copy(w2_bf[:], w2_raw[:].rearrange("p j n -> p n j"))
         nc.vector.quantize_mx(
             out=w2_codes[:].bitcast(FP8X4), scales=w2_scales[:], in_=w2_bf[:].rearrange("p n j -> p (n j)")
         )
 
         ct = [keep.tile([P, 2, P, 2], BF16, name=f"ct{b}", align_bytes=64) for b in range(T // P)]
 
-        def combine(t0, width):
+        wide = {}
+
+        def combine(t0, width, banks):
             sums = {}
             for a in range(CHUNKS):
                 prods = []
                 for r in range(2):
-                    prod = keep.tile([P, width], F32, name=f"prod{t0}_{a}_{r}", align_bytes=64)
+                    if t0 == 0 or a == CHUNKS - 1:
+                        prod = keep.tile([P, width], F32, name=f"prod{t0}_{a}_{r}", align_bytes=64)[:]
+                        wide[a, r] = prod
+                    else:
+                        prod = wide[CHUNKS - 2, r][:, a * P : (a + 1) * P]
                     nc.vector.tensor_tensor(
-                        prod[:],
+                        prod,
                         h[a][:].indirect(pos_sb[r][:, t0 // 16 : (t0 + width) // 16]),
                         gate_sb[:, r, t0 : t0 + width],
                         MULT,
@@ -156,7 +175,7 @@ def tile_moe_sdn_lin_relu_kernel(
                 first = 0 if a < CHUNKS - 1 else a
                 for b in range(width // P):
                     if a == first:
-                        sums[b] = bank()
+                        sums[b] = bank(banks[a == CHUNKS - 1][b])
                     for r in range(2):
                         nc.tensor.matmul(
                             sums[b][:, (a - first) * P : (a - first + 1) * P],
@@ -175,7 +194,7 @@ def tile_moe_sdn_lin_relu_kernel(
 
         def turn_back(g):
             t0, width = GROUPS[g]
-            back = bank()
+            back = bank((6, 7, 0)[g])
             for b in range(width // P):
                 words = ct[t0 // P + b][:].rearrange("t u p e -> t (u p e)").bitcast(F32)
                 for u in range(2):
@@ -194,7 +213,7 @@ def tile_moe_sdn_lin_relu_kernel(
             codes = keep.tile([P, width], U32, name=f"c_codes{g}", align_bytes=64)
             scales = keep.tile([P, width], U8, name=f"c_scales{g}", align_bytes=64)
             nc.vector.quantize_mx(out=codes[:].bitcast(FP8X4), scales=scales[:], in_=c_bf[:])
-            proj = bank()
+            proj = bank(1 + g)
             nc.tensor.matmul_mx(
                 out=proj[:, :width],
                 lhsT=w2_codes[:].bitcast(FP8X4),
@@ -209,8 +228,8 @@ def tile_moe_sdn_lin_relu_kernel(
             nc.sync.dma_start(out[:, t0 : t0 + width], res[:])
 
         rounded = []
-        for t0, width in GATHERS:
-            combine(t0, width)
+        for (t0, width), banks in zip(GATHERS, (((6, 7, 0), (1, 2, 3)), ((4,), (5,)))):
+            combine(t0, width, banks)
             rounded.extend(turn_back(g) for g in range(len(GROUPS)) if t0 <= GROUPS[g][0] < t0 + width)
         for g in range(len(GROUPS)):
             project(g, rounded[g])

@@ -52,10 +52,10 @@ def tile_moe_sdn_lin_relu_kernel(
         gate_sb = keep.tile([P, 2, T], F32, name="gate_sb", align_bytes=64)
         w2_raw = keep.tile([P, 4, N], F32, name="w2_raw", align_bytes=64)
 
-        nc.gpsimd.memset(xs[:].bitcast(I32), 0)
+        nc.vector.memset(xs[:].bitcast(I32), 0)
+        nc.vector.memset(ws[:].bitcast(I32), 0)
         for s in range(PASSES):
             nc.vector.memset(xw[s][:, T:], 0)
-        nc.vector.memset(ws[:].bitcast(I32), 0)
 
         def load_w1(tile, experts, cols):
             nc.sync.dma_start(
@@ -74,12 +74,12 @@ def tile_moe_sdn_lin_relu_kernel(
                 xs[32 * q + X_LEVEL : 32 * q + X_LEVEL + 8, :T].bitcast(I32),
                 x_scales[:, 4 * q : 4 * q + 4, :].bitcast(I32),
             )
-        load_x_words(1)
-        load_w1(ww_early[0], slice(0, 2), slice(0, H // 2))
-        nc.sync.dma_start(gate_row[:], gate[:, 0, :].rearrange("r (n m) -> n r m", m=4))
-        load_w1(ww_early[1], slice(2, 4), slice(0, H // 2))
         for r in range(4):
             nc.sync.dma_start(ws[r:P:32, :].bitcast(I32).rearrange("q (g i) -> q g i", g=E * PASSES), rows[r])
+        nc.sync.dma_start(gate_row[:], gate[:, 0, :].rearrange("r (n m) -> n r m", m=4))
+        load_w1(ww_early[0], slice(0, 2), slice(0, H // 2))
+        load_x_words(1)
+        load_w1(ww_early[1], slice(2, 4), slice(0, H // 2))
         nc.sync.dma_start(w2_raw[:], w2.rearrange("(p j) n -> p j n", j=4))
         nc.sync.dma_start(pos_sb[0][:], pos1)
         nc.sync.dma_start(pos_sb[1][:], pos2)
@@ -124,7 +124,9 @@ def tile_moe_sdn_lin_relu_kernel(
                     start=(s == 0),
                     stop=(s == PASSES - 1),
                 )
-                if s == PASSES - 1:
+                if s == PASSES - 1 and hi - lo < C:
+                    nc.vector.tensor_scalar_max(h[a][:, lo:hi], acc[a, lo][:, : hi - lo], 0.0)
+                elif s == PASSES - 1:
                     nc.scalar.activation(h[a][:, lo:hi], acc[a, lo][:, : hi - lo], RELU)
 
         gather_words(0, 0, S)
@@ -137,9 +139,9 @@ def tile_moe_sdn_lin_relu_kernel(
         whole = [(e * C, (e + 1) * C) for e in range(E)]
         first = whole[:3] + [(3 * C, 3 * C + P), (3 * C + P, S)]
         hidden([(a, 0, lo, hi) for a in range(2) for lo, hi in whole[:2]])
-        hidden([(0, 0, lo, hi) for lo, hi in first[2:]] + [(1, 0, *whole[2])])
+        hidden([(0, 0, lo, hi) for lo, hi in first[2:]])
         hidden([(0, 1, lo, hi) for lo, hi in first])
-        hidden([(1, 1, lo, hi) for lo, hi in whole[:3]] + [(1, s, *whole[3]) for s in range(PASSES)])
+        hidden([(1, 1, lo, hi) for lo, hi in whole[:2]] + [(1, s, lo, hi) for lo, hi in whole[2:] for s in range(PASSES)])
         for a in range(2, CHUNKS):
             hidden([(a, s, lo, hi) for lo, hi in whole for s in range(PASSES)])
 
@@ -160,11 +162,11 @@ def tile_moe_sdn_lin_relu_kernel(
             for a in range(CHUNKS):
                 prods = []
                 for r in range(2):
-                    if t0 == 0 or a == CHUNKS - 1:
+                    if t0 == 0:
                         prod = keep.tile([P, width], F32, name=f"prod{t0}_{a}_{r}", align_bytes=64)[:]
                         wide[a, r] = prod
                     else:
-                        prod = wide[CHUNKS - 2, r][:, a * P : (a + 1) * P]
+                        prod = wide[CHUNKS - 2 + a // 3, r][:, a % 3 * P : (a % 3 + 1) * P]
                     nc.vector.tensor_tensor(
                         prod,
                         h[a][:].indirect(pos_sb[r][:, t0 // 16 : (t0 + width) // 16]),

@@ -22,7 +22,7 @@ PASSES = K // 512
 CHUNKS = H // P
 BANK = 512
 X_LEVEL = 8
-WORD_WINDOW = (1408, 704)
+WORD_WINDOW = 704
 BYTE_WINDOW = 704
 GATHERS = ((0, 384), (384, 128))
 GROUPS = ((0, 256), (256, 128), (384, 128))
@@ -44,8 +44,8 @@ def tile_moe_sdn_lin_relu_kernel(
         pos_sb = [lists.tile([P, T // 16], U16, name=f"pos_sb{r}") for r in range(2)]
 
         xs = keep.tile([P, BYTE_WINDOW], U8, name="xs", align_bytes=64)
-        ws = keep.tile([P, E * PASSES * H], U8, name="ws", align_bytes=64)
-        xw = [keep.tile([P, WORD_WINDOW[s]], I32, name=f"xw{s}", align_bytes=64) for s in range(PASSES)]
+        ws = [keep.tile([P, E * PASSES * H // 2], U8, name=f"ws{half}", align_bytes=64) for half in range(2)]
+        xw = [keep.tile([P, WORD_WINDOW], I32, name=f"xw{s}", align_bytes=64) for s in range(PASSES)]
         ww_early = [keep.tile([P, 2 * PASSES, H // 2], I32, name=f"ww_early{pair}", align_bytes=64) for pair in range(2)]
         ww_late = keep.tile([P, E * PASSES, H // 2], I32, name="ww_late", align_bytes=64)
         gate_row = keep.tile([P, 2, 4], F32, name="gate_row", align_bytes=64)
@@ -53,37 +53,43 @@ def tile_moe_sdn_lin_relu_kernel(
         w2_raw = keep.tile([P, 4, N], F32, name="w2_raw", align_bytes=64)
 
         nc.vector.memset(xs[:].bitcast(I32), 0)
-        nc.vector.memset(ws[:].bitcast(I32), 0)
+        nc.vector.memset(ws[0][:].bitcast(I32), 0)
         for s in range(PASSES):
             nc.vector.memset(xw[s][:, T:], 0)
+        nc.vector.memset(ws[1][:].bitcast(I32), 0)
 
         def load_w1(tile, experts, cols):
             nc.sync.dma_start(
                 tile[:], w1_words[experts, :, :, cols, :].rearrange("e s p i d -> p (e s) (i d)").bitcast(I32)
             )
 
-        rows = w1_scales.rearrange("e s (q r) i -> r q (e s) i", r=4).bitcast(I32)
+        def load_w1_scales(half):
+            rows = w1_scales.rearrange("e s (q r) (c i) -> c r q (e s) i", r=4, c=2).bitcast(I32)[half]
+            for r in range(4):
+                nc.sync.dma_start(
+                    ws[half][r:P:32, :].bitcast(I32).rearrange("q (g i) -> q g i", g=E * PASSES), rows[r]
+                )
 
         def load_x_words(s):
             nc.sync.dma_start(xw[s][:, :T], x_words[s].rearrange("p t d -> p (t d)").bitcast(I32))
 
-        nc.sync.dma_start(offs_sb[:], offs)
         load_x_words(0)
+        nc.sync.dma_start(offs_sb[:], offs)
         for q in range(4):
             nc.sync.dma_start(
                 xs[32 * q + X_LEVEL : 32 * q + X_LEVEL + 8, :T].bitcast(I32),
                 x_scales[:, 4 * q : 4 * q + 4, :].bitcast(I32),
             )
-        for r in range(4):
-            nc.sync.dma_start(ws[r:P:32, :].bitcast(I32).rearrange("q (g i) -> q g i", g=E * PASSES), rows[r])
-        nc.sync.dma_start(gate_row[:], gate[:, 0, :].rearrange("r (n m) -> n r m", m=4))
         load_w1(ww_early[0], slice(0, 2), slice(0, H // 2))
-        load_x_words(1)
+        nc.sync.dma_start(gate_row[:], gate[:, 0, :].rearrange("r (n m) -> n r m", m=4))
+        load_w1_scales(0)
         load_w1(ww_early[1], slice(2, 4), slice(0, H // 2))
-        nc.sync.dma_start(w2_raw[:], w2.rearrange("(p j) n -> p j n", j=4))
         nc.sync.dma_start(pos_sb[0][:], pos1)
         nc.sync.dma_start(pos_sb[1][:], pos2)
+        load_x_words(1)
+        nc.sync.dma_start(w2_raw[:], w2.rearrange("(p j) n -> p j n", j=4))
         load_w1(ww_late, slice(0, E), slice(H // 2, H))
+        load_w1_scales(1)
 
         ident_raw = keep.tile([P, P], F32, name="ident_raw")
         ident = keep.tile([P, P], F32, name="ident")
@@ -114,22 +120,22 @@ def tile_moe_sdn_lin_relu_kernel(
                 e = lo // C
                 if s == 0:
                     acc[a, lo] = bank(len(acc) % 8)
+                byte0 = (PASSES * e + s) * H // 2 + a % 2 * P
                 words = ww_early[e // 2][:, PASSES * (e % 2) + s] if a < 2 else ww_late[:, PASSES * e + s]
                 nc.tensor.matmul_mx(
                     out=acc[a, lo][:, : hi - lo],
                     lhsT=words[:, (a % 2) * P : (a % 2 + 1) * P].bitcast(FP8X4),
-                    lhsT_scale=ws[:, (PASSES * e + s) * H + a * P : (PASSES * e + s) * H + (a + 1) * P],
+                    lhsT_scale=ws[a // 2][:, byte0 : byte0 + P],
                     rhs=gw[s][:, lo:hi].bitcast(FP8X4),
                     rhs_scale=gs[X_LEVEL + 4 * s : P, lo:hi],
                     start=(s == 0),
                     stop=(s == PASSES - 1),
                 )
-                if s == PASSES - 1 and hi - lo < C:
-                    nc.vector.tensor_scalar_max(h[a][:, lo:hi], acc[a, lo][:, : hi - lo], 0.0)
-                elif s == PASSES - 1:
+                if s == PASSES - 1:
                     nc.scalar.activation(h[a][:, lo:hi], acc[a, lo][:, : hi - lo], RELU)
 
-        gather_words(0, 0, S)
+        gather_words(0, 0, 2 * C)
+        gather_words(0, 2 * C, S)
         for lo in (0, 2 * C):
             nc.vector.tensor_copy(gs[:, lo : lo + 2 * C], xs[:].indirect(offs_sb[:, lo // 16 : (lo + 2 * C) // 16]))
         gather_words(1, 0, 2 * C)

@@ -22,9 +22,10 @@ PASSES = K // 512
 CHUNKS = H // P
 BANK = 512
 X_LEVEL = 8
-WORD_WINDOW = 704
+WORD_WINDOW = 1408
+HALF_WINDOW = 704
 BYTE_WINDOW = 704
-GATHERS = ((0, 384), (384, 128))
+HALF = T // 2
 GROUPS = ((0, 256), (256, 128), (384, 128))
 
 
@@ -43,9 +44,9 @@ def tile_moe_sdn_lin_relu_kernel(
         offs_sb = lists.tile([P, S // 16], U16, name="offs_sb")
         pos_sb = [lists.tile([P, T // 16], U16, name=f"pos_sb{r}") for r in range(2)]
 
-        xs = keep.tile([P, BYTE_WINDOW], U8, name="xs", align_bytes=64)
+        xs = keep.tile([P, BYTE_WINDOW + 4], U8, name="xs", align_bytes=64)
         ws = [keep.tile([P, E * PASSES * H // 2], U8, name=f"ws{half}", align_bytes=64) for half in range(2)]
-        xw = [keep.tile([P, WORD_WINDOW], I32, name=f"xw{s}", align_bytes=64) for s in range(PASSES)]
+        xw = keep.tile([P, T + WORD_WINDOW + 1], I32, name="xw", align_bytes=64)
         ww_early = [keep.tile([P, 2 * PASSES, H // 2], I32, name=f"ww_early{pair}", align_bytes=64) for pair in range(2)]
         ww_late = keep.tile([P, E * PASSES, H // 2], I32, name="ww_late", align_bytes=64)
         gate_row = keep.tile([P, 2, 4], F32, name="gate_row", align_bytes=64)
@@ -53,10 +54,8 @@ def tile_moe_sdn_lin_relu_kernel(
         w2_raw = keep.tile([P, 4, N], F32, name="w2_raw", align_bytes=64)
 
         nc.vector.memset(xs[:].bitcast(I32), 0)
-        nc.vector.memset(ws[0][:].bitcast(I32), 0)
-        for s in range(PASSES):
-            nc.vector.memset(xw[s][:, T:], 0)
-        nc.vector.memset(ws[1][:].bitcast(I32), 0)
+        nc.vector.memset(xw[:, PASSES * T :], 0)
+        nc.gpsimd.memset(ws[0][:].bitcast(I32), 0)
 
         def load_w1(tile, experts, cols):
             nc.sync.dma_start(
@@ -71,7 +70,7 @@ def tile_moe_sdn_lin_relu_kernel(
                 )
 
         def load_x_words(s):
-            nc.sync.dma_start(xw[s][:, :T], x_words[s].rearrange("p t d -> p (t d)").bitcast(I32))
+            nc.sync.dma_start(xw[:, (1 - s) * T : (2 - s) * T], x_words[s].rearrange("p t d -> p (t d)").bitcast(I32))
 
         load_x_words(0)
         nc.sync.dma_start(offs_sb[:], offs)
@@ -89,11 +88,12 @@ def tile_moe_sdn_lin_relu_kernel(
         load_x_words(1)
         nc.sync.dma_start(w2_raw[:], w2.rearrange("(p j) n -> p j n", j=4))
         load_w1(ww_late, slice(0, E), slice(H // 2, H))
-        load_w1_scales(1)
 
         ident_raw = keep.tile([P, P], F32, name="ident_raw")
         ident = keep.tile([P, P], F32, name="ident")
         make_identity(nc, ident_raw[:])
+        nc.gpsimd.memset(ws[1][:].bitcast(I32), 0)
+        load_w1_scales(1)
         nc.scalar.activation(ident[:], ident_raw[:], RELU)
 
         for r in range(2):
@@ -110,46 +110,58 @@ def tile_moe_sdn_lin_relu_kernel(
         gs = keep.tile([P, S], U8, name="gs", align_bytes=64)
         gw = [keep.tile([P, S], U32, name=f"gw{s}", align_bytes=64) for s in range(PASSES)]
 
-        def gather_words(s, lo, hi):
-            nc.vector.tensor_copy(gw[s][:, lo:hi], xw[s][:].bitcast(U32).indirect(offs_sb[:, lo // 16 : hi // 16]))
+        def gather_words(s, lo, hi, window):
+            first = (1 - s) * T
+            nc.vector.tensor_copy(
+                gw[s][:, lo:hi], xw[:, first : first + window].bitcast(U32).indirect(offs_sb[:, lo // 16 : hi // 16])
+            )
+
+        def product(acc, col, a, s, lo, hi, start, stop):
+            e = lo // C
+            byte0 = (PASSES * e + s) * H // 2 + a % 2 * P
+            words = ww_early[e // 2][:, PASSES * (e % 2) + s] if a < 2 else ww_late[:, PASSES * e + s]
+            nc.tensor.matmul_mx(
+                out=acc[:, col : col + hi - lo],
+                lhsT=words[:, (a % 2) * P : (a % 2 + 1) * P].bitcast(FP8X4),
+                lhsT_scale=ws[a // 2][:, byte0 : byte0 + P],
+                rhs=gw[s][:, lo:hi].bitcast(FP8X4),
+                rhs_scale=gs[X_LEVEL + 4 * s : P, lo:hi],
+                start=start,
+                stop=stop,
+            )
 
         acc = {}
 
-        def hidden(steps):
-            for a, s, lo, hi in steps:
-                e = lo // C
-                if s == 0:
-                    acc[a, lo] = bank(len(acc) % 8)
-                byte0 = (PASSES * e + s) * H // 2 + a % 2 * P
-                words = ww_early[e // 2][:, PASSES * (e % 2) + s] if a < 2 else ww_late[:, PASSES * e + s]
-                nc.tensor.matmul_mx(
-                    out=acc[a, lo][:, : hi - lo],
-                    lhsT=words[:, (a % 2) * P : (a % 2 + 1) * P].bitcast(FP8X4),
-                    lhsT_scale=ws[a // 2][:, byte0 : byte0 + P],
-                    rhs=gw[s][:, lo:hi].bitcast(FP8X4),
-                    rhs_scale=gs[X_LEVEL + 4 * s : P, lo:hi],
-                    start=(s == 0),
-                    stop=(s == PASSES - 1),
-                )
-                if s == PASSES - 1:
-                    nc.scalar.activation(h[a][:, lo:hi], acc[a, lo][:, : hi - lo], RELU)
+        def open_sums(a, lo, hi, n):
+            acc[a, lo] = bank(n)
+            for e0 in range(lo, hi, C):
+                product(acc[a, lo], e0 - lo, a, 0, e0, min(hi, e0 + C), e0 == lo, False)
 
-        gather_words(0, 0, 2 * C)
-        gather_words(0, 2 * C, S)
+        def close_sums(a, lo, hi):
+            for e0 in range(lo, hi, C):
+                product(acc[a, lo], e0 - lo, a, 1, e0, min(hi, e0 + C), False, e0 + C >= hi)
+            nc.scalar.activation(h[a][:, lo:hi], acc[a, lo][:, : hi - lo], RELU)
+
+        gather_words(0, 0, S, WORD_WINDOW)
         for lo in (0, 2 * C):
-            nc.vector.tensor_copy(gs[:, lo : lo + 2 * C], xs[:].indirect(offs_sb[:, lo // 16 : (lo + 2 * C) // 16]))
-        gather_words(1, 0, 2 * C)
-        gather_words(1, 2 * C, 3 * C)
-        gather_words(1, 3 * C, 3 * C + P)
-        gather_words(1, 3 * C + P, S)
-        whole = [(e * C, (e + 1) * C) for e in range(E)]
-        first = whole[:3] + [(3 * C, 3 * C + P), (3 * C + P, S)]
-        hidden([(a, 0, lo, hi) for a in range(2) for lo, hi in whole[:2]])
-        hidden([(0, 0, lo, hi) for lo, hi in first[2:]])
-        hidden([(0, 1, lo, hi) for lo, hi in first])
-        hidden([(1, 1, lo, hi) for lo, hi in whole[:2]] + [(1, s, lo, hi) for lo, hi in whole[2:] for s in range(PASSES)])
+            nc.vector.tensor_copy(gs[:, lo : lo + 2 * C], xs[:, :BYTE_WINDOW].indirect(offs_sb[:, lo // 16 : (lo + 2 * C) // 16]))
+        pieces = [(0, 2 * C), (2 * C, 3 * C), (3 * C, 3 * C + P), (3 * C + P, S)]
+        halves = [(0, 2 * C), (2 * C, S)]
+        for lo, hi in pieces:
+            gather_words(1, lo, hi, HALF_WINDOW if hi - lo == 2 * C else T)
+        open_sums(0, *pieces[0], 0)
+        open_sums(1, *halves[0], 4)
+        for n in range(1, 4):
+            open_sums(0, *pieces[n], n)
+        open_sums(1, *halves[1], 5)
+        for lo, hi in pieces:
+            close_sums(0, lo, hi)
+        for lo, hi in halves:
+            close_sums(1, lo, hi)
         for a in range(2, CHUNKS):
-            hidden([(a, s, lo, hi) for lo, hi in whole for s in range(PASSES)])
+            for n, (lo, hi) in enumerate(halves):
+                open_sums(a, lo, hi, (2 * a + 2 + n) % 8)
+                close_sums(a, lo, hi)
 
         w2_bf = keep.tile([P, N, 4], BF16, name="w2_bf", align_bytes=64)
         w2_codes = keep.tile([P, N], U32, name="w2_codes", align_bytes=64)
@@ -159,52 +171,43 @@ def tile_moe_sdn_lin_relu_kernel(
             out=w2_codes[:].bitcast(FP8X4), scales=w2_scales[:], in_=w2_bf[:].rearrange("p n j -> p (n j)")
         )
 
-        ct = [keep.tile([P, 2, P, 2], BF16, name=f"ct{b}", align_bytes=64) for b in range(T // P)]
+        ct = keep.tile([P, T // P * H], BF16, name="ct", align_bytes=64)
 
-        wide = {}
+        prods = [[keep.tile([P, T], F32, name=f"prod{n}_{r}", align_bytes=64) for r in range(2)] for n in range(3)]
 
-        def combine(t0, width, banks):
-            sums = {}
-            for a in range(CHUNKS):
-                prods = []
+        def gated(a, t0, width, tiles, col):
+            for r in range(2):
+                nc.vector.tensor_tensor(
+                    tiles[r][:, col : col + width],
+                    h[a][:].indirect(pos_sb[r][:, t0 // 16 : (t0 + width) // 16]),
+                    gate_sb[:, r, t0 : t0 + width],
+                    MULT,
+                )
+
+        def add_turned(sums, tiles, col, r):
+            nc.tensor.matmul(
+                sums, lhsT=tiles[r][:, col : col + P], rhs=ident[:], start=(r == 0), stop=(r == 1), is_transpose=True
+            )
+
+        def round_sums(a, t0, sums):
+            width = sums.shape[1]
+            blocks = ct[:, t0 // P * H : (t0 + width) // P * H].rearrange("t (b u p e) -> t b u p e", u=2, p=P, e=2)
+            nc.scalar.copy(
+                blocks[:, :, :, 32 * a : 32 * (a + 1), :], sums.rearrange("t (b p u e) -> t b u p e", p=32, u=2, e=2)
+            )
+
+        def combine(a, t0, width, tiles, col, sums):
+            gated(a, t0, width, tiles, col)
+            for b in range(width // P):
                 for r in range(2):
-                    if t0 == 0:
-                        prod = keep.tile([P, width], F32, name=f"prod{t0}_{a}_{r}", align_bytes=64)[:]
-                        wide[a, r] = prod
-                    else:
-                        prod = wide[CHUNKS - 2 + a // 3, r][:, a % 3 * P : (a % 3 + 1) * P]
-                    nc.vector.tensor_tensor(
-                        prod,
-                        h[a][:].indirect(pos_sb[r][:, t0 // 16 : (t0 + width) // 16]),
-                        gate_sb[:, r, t0 : t0 + width],
-                        MULT,
-                    )
-                    prods.append(prod)
-                first = 0 if a < CHUNKS - 1 else a
-                for b in range(width // P):
-                    if a == first:
-                        sums[b] = bank(banks[a == CHUNKS - 1][b])
-                    for r in range(2):
-                        nc.tensor.matmul(
-                            sums[b][:, (a - first) * P : (a - first + 1) * P],
-                            lhsT=prods[r][:, b * P : (b + 1) * P],
-                            rhs=ident[:],
-                            start=(r == 0),
-                            stop=(r == 1),
-                            is_transpose=True,
-                        )
-                    if a >= CHUNKS - 2:
-                        n = a - first + 1
-                        nc.scalar.copy(
-                            ct[t0 // P + b][:, :, 32 * first : 32 * (a + 1), :],
-                            sums[b][:, : n * P].rearrange("t (p u e) -> t u p e", u=2, e=2),
-                        )
+                    add_turned(sums[:, b * P : (b + 1) * P], tiles, col + b * P, r)
+            round_sums(a, t0, sums)
 
         def turn_back(g):
             t0, width = GROUPS[g]
-            back = bank((6, 7, 0)[g])
+            back = bank((6, 3, 4)[g])
             for b in range(width // P):
-                words = ct[t0 // P + b][:].rearrange("t u p e -> t (u p e)").bitcast(F32)
+                words = ct[:, (t0 // P + b) * H : (t0 // P + b + 1) * H].bitcast(F32)
                 for u in range(2):
                     nc.tensor.transpose(
                         back[:, u * width + b * P : u * width + (b + 1) * P], words[:, u * P : (u + 1) * P], ident[:]
@@ -221,7 +224,7 @@ def tile_moe_sdn_lin_relu_kernel(
             codes = keep.tile([P, width], U32, name=f"c_codes{g}", align_bytes=64)
             scales = keep.tile([P, width], U8, name=f"c_scales{g}", align_bytes=64)
             nc.vector.quantize_mx(out=codes[:].bitcast(FP8X4), scales=scales[:], in_=c_bf[:])
-            proj = bank(1 + g)
+            proj = bank((2, 5, 1)[g])
             nc.tensor.matmul_mx(
                 out=proj[:, :width],
                 lhsT=w2_codes[:].bitcast(FP8X4),
@@ -232,12 +235,27 @@ def tile_moe_sdn_lin_relu_kernel(
                 stop=True,
             )
             res = keep.tile([P, width], F32, name=f"res{g}", align_bytes=64)
-            nc.vector.tensor_copy(res[:], proj[:, :width])
+            if g < len(GROUPS) - 1:
+                nc.scalar.copy(res[:], proj[:, :width])
+            else:
+                nc.vector.tensor_copy(res[:], proj[:, :width])
             nc.sync.dma_start(out[:, t0 : t0 + width], res[:])
 
-        rounded = []
-        for (t0, width), banks in zip(GATHERS, (((6, 7, 0), (1, 2, 3)), ((4,), (5,)))):
-            combine(t0, width, banks)
-            rounded.extend(turn_back(g) for g in range(len(GROUPS)) if t0 <= GROUPS[g][0] < t0 + width)
+        combine(0, 0, T, prods[0], 0, bank(7)[:])
+        combine(1, 0, T, prods[1], 0, bank(1)[:])
+        combine(2, 0, HALF, prods[2], 0, bank(7)[:, :HALF])
+        gated(3, 0, HALF, prods[2], HALF)
+        closing = [bank(0), bank(2)]
+        for r in range(2):
+            for b in range(2):
+                add_turned(closing[b][:, :P], prods[2], HALF + b * P, r)
+        for b in range(2):
+            round_sums(3, b * P, closing[b][:, :P])
+        rounded = [turn_back(0)]
+        combine(2, HALF, HALF, prods[1], 0, bank(0)[:, :HALF])
+        last = bank(2)
+        for b in range(2):
+            combine(3, HALF + b * P, P, prods[1], HALF + b * P, last[:, b * P : (b + 1) * P])
+        rounded.extend(turn_back(g) for g in (1, 2))
         for g in range(len(GROUPS)):
             project(g, rounded[g])

@@ -44,9 +44,9 @@ def tile_moe_sdn_lin_relu_kernel(
         offs_sb = lists.tile([P, S // 16], U16, name="offs_sb")
         pos_sb = [lists.tile([P, T // 16], U16, name=f"pos_sb{r}") for r in range(2)]
 
-        xs = keep.tile([P, BYTE_WINDOW + 4], U8, name="xs", align_bytes=64)
+        xs = keep.tile([P, BYTE_WINDOW], U8, name="xs", align_bytes=64)
         ws = [keep.tile([P, E * PASSES * H // 2], U8, name=f"ws{half}", align_bytes=64) for half in range(2)]
-        xw = keep.tile([P, T + WORD_WINDOW + 1], I32, name="xw", align_bytes=64)
+        xw = keep.tile([P, T + WORD_WINDOW], I32, name="xw", align_bytes=64)
         ww_early = [keep.tile([P, 2 * PASSES, H // 2], I32, name=f"ww_early{pair}", align_bytes=64) for pair in range(2)]
         ww_late = keep.tile([P, E * PASSES, H // 2], I32, name="ww_late", align_bytes=64)
         gate_row = keep.tile([P, 2, 4], F32, name="gate_row", align_bytes=64)
@@ -54,8 +54,9 @@ def tile_moe_sdn_lin_relu_kernel(
         w2_raw = keep.tile([P, 4, N], F32, name="w2_raw", align_bytes=64)
 
         nc.vector.memset(xs[:].bitcast(I32), 0)
+        nc.vector.memset(ws[0][:].bitcast(I32), 0)
         nc.vector.memset(xw[:, PASSES * T :], 0)
-        nc.gpsimd.memset(ws[0][:].bitcast(I32), 0)
+        nc.vector.memset(ws[1][:].bitcast(I32), 0)
 
         def load_w1(tile, experts, cols):
             nc.sync.dma_start(
@@ -92,7 +93,6 @@ def tile_moe_sdn_lin_relu_kernel(
         ident_raw = keep.tile([P, P], F32, name="ident_raw")
         ident = keep.tile([P, P], F32, name="ident")
         make_identity(nc, ident_raw[:])
-        nc.gpsimd.memset(ws[1][:].bitcast(I32), 0)
         load_w1_scales(1)
         nc.scalar.activation(ident[:], ident_raw[:], RELU)
 
@@ -144,7 +144,7 @@ def tile_moe_sdn_lin_relu_kernel(
 
         gather_words(0, 0, S, WORD_WINDOW)
         for lo in (0, 2 * C):
-            nc.vector.tensor_copy(gs[:, lo : lo + 2 * C], xs[:, :BYTE_WINDOW].indirect(offs_sb[:, lo // 16 : (lo + 2 * C) // 16]))
+            nc.vector.tensor_copy(gs[:, lo : lo + 2 * C], xs[:].indirect(offs_sb[:, lo // 16 : (lo + 2 * C) // 16]))
         pieces = [(0, 2 * C), (2 * C, 3 * C), (3 * C, 3 * C + P), (3 * C + P, S)]
         halves = [(0, 2 * C), (2 * C, S)]
         for lo, hi in pieces:

@@ -184,9 +184,9 @@ def tile_moe_sdn_lin_relu_kernel(
                     MULT,
                 )
 
-        def add_turned(sums, tiles, col, r):
+        def add_turned(sums, tiles, col, r, start, stop):
             nc.tensor.matmul(
-                sums, lhsT=tiles[r][:, col : col + P], rhs=ident[:], start=(r == 0), stop=(r == 1), is_transpose=True
+                sums, lhsT=tiles[r][:, col : col + P], rhs=ident[:], start=start, stop=stop, is_transpose=True
             )
 
         def round_sums(a, t0, sums):
@@ -198,14 +198,17 @@ def tile_moe_sdn_lin_relu_kernel(
 
         def combine(a, t0, width, tiles, col, sums):
             gated(a, t0, width, tiles, col)
-            for b in range(width // P):
-                for r in range(2):
-                    add_turned(sums[:, b * P : (b + 1) * P], tiles, col + b * P, r)
+            blocks = width // P
+            for r in range(2):
+                for b in range(blocks):
+                    add_turned(
+                        sums[:, b * P : (b + 1) * P], tiles, col + b * P, r, r + b == 0, r == 1 and b == blocks - 1
+                    )
             round_sums(a, t0, sums)
 
         def turn_back(g):
             t0, width = GROUPS[g]
-            back = bank((6, 3, 4)[g])
+            back = bank((6, 5, 1)[g])
             for b in range(width // P):
                 words = ct[:, (t0 // P + b) * H : (t0 // P + b + 1) * H].bitcast(F32)
                 for u in range(2):
@@ -213,7 +216,7 @@ def tile_moe_sdn_lin_relu_kernel(
                         back[:, u * width + b * P : u * width + (b + 1) * P], words[:, u * P : (u + 1) * P], ident[:]
                     )
             c_bf = keep.tile([P, width * 4], BF16, name=f"c_bf{g}", align_bytes=64)
-            nc.scalar.copy(
+            (nc.vector.tensor_copy if g == 0 else nc.scalar.copy)(
                 c_bf[:].bitcast(F32).rearrange("p (t u) -> p t u", u=2),
                 back[:, : 2 * width].rearrange("p (u t) -> p t u", u=2),
             )
@@ -224,7 +227,7 @@ def tile_moe_sdn_lin_relu_kernel(
             codes = keep.tile([P, width], U32, name=f"c_codes{g}", align_bytes=64)
             scales = keep.tile([P, width], U8, name=f"c_scales{g}", align_bytes=64)
             nc.vector.quantize_mx(out=codes[:].bitcast(FP8X4), scales=scales[:], in_=c_bf[:])
-            proj = bank((2, 5, 1)[g])
+            proj = bank((2, 3, 4)[g])
             nc.tensor.matmul_mx(
                 out=proj[:, :width],
                 lhsT=w2_codes[:].bitcast(FP8X4),
@@ -248,14 +251,13 @@ def tile_moe_sdn_lin_relu_kernel(
         closing = [bank(0), bank(2)]
         for r in range(2):
             for b in range(2):
-                add_turned(closing[b][:, :P], prods[2], HALF + b * P, r)
+                add_turned(closing[b][:, :P], prods[2], HALF + b * P, r, r == 0, r == 1)
         for b in range(2):
             round_sums(3, b * P, closing[b][:, :P])
         rounded = [turn_back(0)]
-        combine(2, HALF, HALF, prods[1], 0, bank(0)[:, :HALF])
-        last = bank(2)
+        combine(2, HALF, HALF, prods[1], 0, bank(3)[:, :HALF])
         for b in range(2):
-            combine(3, HALF + b * P, P, prods[1], HALF + b * P, last[:, b * P : (b + 1) * P])
+            combine(3, HALF + b * P, P, prods[1], HALF + b * P, bank(2 * b)[:, :P])
         rounded.extend(turn_back(g) for g in (1, 2))
         for g in range(len(GROUPS)):
             project(g, rounded[g])

@@ -206,6 +206,20 @@ def tile_moe_sdn_lin_relu_kernel(
                     )
             round_sums(a, t0, sums)
 
+        def warmed(n):
+            spare = bank(n)
+            for s in range(PASSES):
+                nc.tensor.matmul_mx(
+                    out=spare[:],
+                    lhsT=ww_late[:, s, :P].bitcast(FP8X4),
+                    lhsT_scale=ws[1][:, s * H // 2 : s * H // 2 + P],
+                    rhs=gw[s][:, :BANK].bitcast(FP8X4),
+                    rhs_scale=gs[X_LEVEL + 4 * s : P, :BANK],
+                    start=(s == 0),
+                    stop=(s == PASSES - 1),
+                )
+            return spare
+
         def turn_back(g):
             t0, width = GROUPS[g]
             back = bank((6, 5, 1)[g])
@@ -246,7 +260,7 @@ def tile_moe_sdn_lin_relu_kernel(
 
         combine(0, 0, T, prods[0], 0, bank(7)[:])
         combine(1, 0, T, prods[1], 0, bank(1)[:])
-        combine(2, 0, HALF, prods[2], 0, bank(7)[:, :HALF])
+        combine(2, 0, HALF, prods[2], 0, warmed(7)[:, :HALF])
         gated(3, 0, HALF, prods[2], HALF)
         closing = [bank(0), bank(2)]
         for r in range(2):
@@ -255,7 +269,7 @@ def tile_moe_sdn_lin_relu_kernel(
         for b in range(2):
             round_sums(3, b * P, closing[b][:, :P])
         rounded = [turn_back(0)]
-        combine(2, HALF, HALF, prods[1], 0, bank(3)[:, :HALF])
+        combine(2, HALF, HALF, prods[1], 0, warmed(7)[:, :HALF])
         for b in range(2):
             combine(3, HALF + b * P, P, prods[1], HALF + b * P, bank(2 * b)[:, :P])
         rounded.extend(turn_back(g) for g in (1, 2))

@@ -158,10 +158,9 @@ def tile_moe_sdn_lin_relu_kernel(
             close_sums(0, lo, hi)
         for lo, hi in halves:
             close_sums(1, lo, hi)
-        for a in range(2, CHUNKS):
-            for n, (lo, hi) in enumerate(halves):
-                open_sums(a, lo, hi, (2 * a + 2 + n) % 8)
-                close_sums(a, lo, hi)
+        for a, (lo, hi), n in ((2, halves[0], 6), (2, halves[1], 7), (3, halves[0], 0)):
+            open_sums(a, lo, hi, n)
+            close_sums(a, lo, hi)
 
         w2_bf = keep.tile([P, N, 4], BF16, name="w2_bf", align_bytes=64)
         w2_codes = keep.tile([P, N], U32, name="w2_codes", align_bytes=64)
@@ -222,7 +221,7 @@ def tile_moe_sdn_lin_relu_kernel(
 
         def turn_back(g):
             t0, width = GROUPS[g]
-            back = bank((6, 5, 1)[g])
+            back = bank((1, 3, 7)[g])
             for b in range(width // P):
                 words = ct[:, (t0 // P + b) * H : (t0 // P + b + 1) * H].bitcast(F32)
                 for u in range(2):
@@ -241,7 +240,7 @@ def tile_moe_sdn_lin_relu_kernel(
             codes = keep.tile([P, width], U32, name=f"c_codes{g}", align_bytes=64)
             scales = keep.tile([P, width], U8, name=f"c_scales{g}", align_bytes=64)
             nc.vector.quantize_mx(out=codes[:].bitcast(FP8X4), scales=scales[:], in_=c_bf[:])
-            proj = bank((2, 3, 4)[g])
+            proj = bank((2, 4, 5)[g])
             nc.tensor.matmul_mx(
                 out=proj[:, :width],
                 lhsT=w2_codes[:].bitcast(FP8X4),
@@ -258,20 +257,30 @@ def tile_moe_sdn_lin_relu_kernel(
                 nc.vector.tensor_copy(res[:], proj[:, :width])
             nc.sync.dma_start(out[:, t0 : t0 + width], res[:])
 
-        combine(0, 0, T, prods[0], 0, bank(7)[:])
-        combine(1, 0, T, prods[1], 0, bank(1)[:])
-        combine(2, 0, HALF, prods[2], 0, warmed(7)[:, :HALF])
+        gated(0, 0, T, prods[0], 0)
+        opening = [bank(6), bank(7)]
+        for r in range(2):
+            for b in range(4):
+                add_turned(
+                    opening[b // 2][:, b % 2 * P : (b % 2 + 1) * P], prods[0], b * P, r, r + b % 2 == 0, r + b % 2 == 2
+                )
+        for n in range(2):
+            round_sums(0, n * HALF, opening[n][:, :HALF])
+        open_sums(3, *halves[1], 6)
+        close_sums(3, *halves[1])
+        combine(1, 0, T, prods[1], 0, bank(7)[:])
+        combine(2, 0, HALF, prods[2], 0, warmed(6)[:, :HALF])
         gated(3, 0, HALF, prods[2], HALF)
-        closing = [bank(0), bank(2)]
+        closing = [bank(7), bank(2)]
         for r in range(2):
             for b in range(2):
                 add_turned(closing[b][:, :P], prods[2], HALF + b * P, r, r == 0, r == 1)
         for b in range(2):
             round_sums(3, b * P, closing[b][:, :P])
         rounded = [turn_back(0)]
-        combine(2, HALF, HALF, prods[1], 0, warmed(7)[:, :HALF])
-        for b in range(2):
-            combine(3, HALF + b * P, P, prods[1], HALF + b * P, bank(2 * b)[:, :P])
+        combine(2, HALF, HALF, prods[1], 0, warmed(6)[:, :HALF])
+        combine(3, HALF, P, prods[1], HALF, bank(7)[:, :P])
+        combine(3, HALF + P, P, prods[1], HALF + P, bank(2)[:, :P])
         rounded.extend(turn_back(g) for g in (1, 2))
         for g in range(len(GROUPS)):
             project(g, rounded[g])

@@ -27,6 +27,7 @@ HALF_WINDOW = 704
 BYTE_WINDOW = 704
 HALF = T // 2
 GROUPS = ((0, 256), (256, 128), (384, 128))
+PARTS = ((0, 256), (256, 128), (384, 64), (448, 64))
 
 
 def tile_moe_sdn_lin_relu_kernel(
@@ -228,19 +229,25 @@ def tile_moe_sdn_lin_relu_kernel(
                     nc.tensor.transpose(
                         back[:, u * width + b * P : u * width + (b + 1) * P], words[:, u * P : (u + 1) * P], ident[:]
                     )
-            c_bf = keep.tile([P, width * 4], BF16, name=f"c_bf{g}", align_bytes=64)
-            (nc.vector.tensor_copy if g == 0 else nc.scalar.copy)(
-                c_bf[:].bitcast(F32).rearrange("p (t u) -> p t u", u=2),
-                back[:, : 2 * width].rearrange("p (u t) -> p t u", u=2),
-            )
-            return c_bf
+            parts = []
+            for p0, n in PARTS:
+                if t0 <= p0 < t0 + width:
+                    c_bf = keep.tile([P, n * 4], BF16, name=f"c_bf{p0}", align_bytes=64)
+                    (nc.vector.tensor_copy if g < 2 else nc.scalar.copy)(
+                        c_bf[:].bitcast(F32).rearrange("p (t u) -> p t u", u=2),
+                        back[:, : 2 * width].rearrange("p (u t) -> p t u", u=2)[:, p0 - t0 : p0 - t0 + n, :],
+                    )
+                    parts.append(c_bf)
+            return parts
+
+        res = keep.tile([P, T], F32, name="res", align_bytes=64)
 
         def project(g, c_bf):
-            t0, width = GROUPS[g]
+            t0, width = PARTS[g]
             codes = keep.tile([P, width], U32, name=f"c_codes{g}", align_bytes=64)
             scales = keep.tile([P, width], U8, name=f"c_scales{g}", align_bytes=64)
             nc.vector.quantize_mx(out=codes[:].bitcast(FP8X4), scales=scales[:], in_=c_bf[:])
-            proj = bank((2, 4, 5)[g])
+            proj = bank((2, 4, 5, 0)[g])
             nc.tensor.matmul_mx(
                 out=proj[:, :width],
                 lhsT=w2_codes[:].bitcast(FP8X4),
@@ -250,12 +257,13 @@ def tile_moe_sdn_lin_relu_kernel(
                 start=True,
                 stop=True,
             )
-            res = keep.tile([P, width], F32, name=f"res{g}", align_bytes=64)
-            if g < len(GROUPS) - 1:
-                nc.scalar.copy(res[:], proj[:, :width])
+            if g == 0:
+                nc.scalar.copy(res[:, t0 : t0 + width], proj[:, :width])
             else:
-                nc.vector.tensor_copy(res[:], proj[:, :width])
-            nc.sync.dma_start(out[:, t0 : t0 + width], res[:])
+                nc.vector.tensor_copy(res[:, t0 : t0 + width], proj[:, :width])
+            for first, n in GROUPS:
+                if first + n == t0 + width:
+                    nc.sync.dma_start(out[:, first : first + n], res[:, first : first + n])
 
         gated(0, 0, T, prods[0], 0)
         opening = [bank(6), bank(7)]
@@ -277,10 +285,11 @@ def tile_moe_sdn_lin_relu_kernel(
                 add_turned(closing[b][:, :P], prods[2], HALF + b * P, r, r == 0, r == 1)
         for b in range(2):
             round_sums(3, b * P, closing[b][:, :P])
-        rounded = [turn_back(0)]
+        rounded = turn_back(0)
         combine(2, HALF, HALF, prods[1], 0, warmed(6)[:, :HALF])
         combine(3, HALF, P, prods[1], HALF, bank(7)[:, :P])
         combine(3, HALF + P, P, prods[1], HALF + P, bank(2)[:, :P])
-        rounded.extend(turn_back(g) for g in (1, 2))
-        for g in range(len(GROUPS)):
+        for g in (1, 2):
+            rounded.extend(turn_back(g))
+        for g in range(len(PARTS)):
             project(g, rounded[g])

@@ -15,19 +15,16 @@ U16 = mybir.dt.uint16
 U8 = mybir.dt.uint8
 FP8X4 = mybir.dt.float8_e4m3fn_x4
 RELU = mybir.ActivationFunctionType.Relu
+COPY = mybir.ActivationFunctionType.Copy
 MULT = mybir.AluOpType.mult
+ADD = mybir.AluOpType.add
 
 P = 128
 PASSES = K // 512
 CHUNKS = H // P
 BANK = 512
 X_LEVEL = 8
-WORD_WINDOW = 1408
-HALF_WINDOW = 704
 BYTE_WINDOW = 704
-HALF = T // 2
-GROUPS = ((0, 256), (256, 128), (384, 128))
-PARTS = ((0, 256), (256, 128), (384, 64), (448, 64))
 
 
 def tile_moe_sdn_lin_relu_kernel(
@@ -42,212 +39,222 @@ def tile_moe_sdn_lin_relu_kernel(
         def bank(n):
             return psum.tile([P, BANK], F32, name=f"bank{n}")
 
+        def held(name, shape, dtype):
+            return keep.tile(shape, dtype, name=name, align_bytes=64)
+
         offs_sb = lists.tile([P, S // 16], U16, name="offs_sb")
         pos_sb = [lists.tile([P, T // 16], U16, name=f"pos_sb{r}") for r in range(2)]
 
-        xs = keep.tile([P, BYTE_WINDOW], U8, name="xs", align_bytes=64)
-        ws = [keep.tile([P, E * PASSES * H // 2], U8, name=f"ws{half}", align_bytes=64) for half in range(2)]
-        xw = keep.tile([P, T + WORD_WINDOW], I32, name="xw", align_bytes=64)
-        ww_early = [keep.tile([P, 2 * PASSES, H // 2], I32, name=f"ww_early{pair}", align_bytes=64) for pair in range(2)]
-        ww_late = keep.tile([P, E * PASSES, H // 2], I32, name="ww_late", align_bytes=64)
-        gate_row = keep.tile([P, 2, 4], F32, name="gate_row", align_bytes=64)
-        gate_sb = keep.tile([P, 2, T], F32, name="gate_sb", align_bytes=64)
-        w2_raw = keep.tile([P, 4, N], F32, name="w2_raw", align_bytes=64)
+        xs = held("xs", [P, BYTE_WINDOW], U8)
+        xw = held("xw", [P, PASSES * T], I32)
+        ws = [held(f"ws{pair}", [P, H], U8) for pair in range(2)]
+        ww = [held(f"ww{e}", [P, PASSES, 3 * P], I32) for e in range(E)]
+        ww_late = [held(f"ww_late{pair}", [P, 2 * PASSES, P], I32) for pair in range(2)]
+        gate_sb = [held(f"gate_sb{half}", [P, 2, T // 2], F32) for half in range(2)]
+        gate_col = [held(f"gate_col{r}", [P, 3], F32) for r in range(2)]
+        w2_raw = held("w2_raw", [P, 4, N], F32)
 
-        nc.vector.memset(xs[:].bitcast(I32), 0)
-        nc.vector.memset(ws[0][:].bitcast(I32), 0)
-        nc.vector.memset(xw[:, PASSES * T :], 0)
-        nc.vector.memset(ws[1][:].bitcast(I32), 0)
+        nc.gpsimd.memset(xs[:].bitcast(I32), 0)
+        for pair in range(2):
+            nc.gpsimd.memset(ws[pair][:].bitcast(I32), 0)
+
+        def load_x_words(s):
+            nc.sync.dma_start(xw[:, s * T : (s + 1) * T], x_words[s].rearrange("p t d -> p (t d)").bitcast(I32))
 
         def load_w1(tile, experts, cols):
             nc.sync.dma_start(
                 tile[:], w1_words[experts, :, :, cols, :].rearrange("e s p i d -> p (e s) (i d)").bitcast(I32)
             )
 
-        def load_w1_scales(half):
-            rows = w1_scales.rearrange("e s (q r) (c i) -> c r q (e s) i", r=4, c=2).bitcast(I32)[half]
-            for r in range(4):
-                nc.sync.dma_start(
-                    ws[half][r:P:32, :].bitcast(I32).rearrange("q (g i) -> q g i", g=E * PASSES), rows[r]
-                )
+        def load_w1_scales(pair):
+            rows = w1_scales.rearrange("(c h) s (q r) i -> c q (h s) r i", h=2, r=4).bitcast(I32)
+            for q in range(4):
+                nc.sync.dma_start(ws[pair][32 * q : 32 * q + 16, :].bitcast(I32), rows[pair, q])
 
-        def load_x_words(s):
-            nc.sync.dma_start(xw[:, (1 - s) * T : (2 - s) * T], x_words[s].rearrange("p t d -> p (t d)").bitcast(I32))
+        def load_gate(half):
+            cols = slice(half * T // 2, (half + 1) * T // 2)
+            nc.sync.dma_start(gate_sb[half][:], gate[:, :, cols].rearrange("r p t -> p r t"))
 
-        load_x_words(0)
-        nc.sync.dma_start(offs_sb[:], offs)
         for q in range(4):
             nc.sync.dma_start(
                 xs[32 * q + X_LEVEL : 32 * q + X_LEVEL + 8, :T].bitcast(I32),
                 x_scales[:, 4 * q : 4 * q + 4, :].bitcast(I32),
             )
-        load_w1(ww_early[0], slice(0, 2), slice(0, H // 2))
-        nc.sync.dma_start(gate_row[:], gate[:, 0, :].rearrange("r (n m) -> n r m", m=4))
-        load_w1_scales(0)
-        load_w1(ww_early[1], slice(2, 4), slice(0, H // 2))
-        nc.sync.dma_start(pos_sb[0][:], pos1)
-        nc.sync.dma_start(pos_sb[1][:], pos2)
+        nc.sync.dma_start(offs_sb[:], offs)
+        load_x_words(0)
         load_x_words(1)
+        load_w1(ww[0], slice(0, 1), slice(0, 3 * P))
+        load_w1_scales(0)
+        load_w1(ww[1], slice(1, 2), slice(0, 3 * P))
+        load_w1(ww[2], slice(2, 3), slice(0, 3 * P))
+        load_w1_scales(1)
+        load_w1(ww[3], slice(3, 4), slice(0, 3 * P))
+        load_w1(ww_late[0], slice(0, 2), slice(3 * P, H))
         nc.sync.dma_start(w2_raw[:], w2.rearrange("(p j) n -> p j n", j=4))
-        load_w1(ww_late, slice(0, E), slice(H // 2, H))
+        load_gate(0)
+        load_gate(1)
+        nc.sync.dma_start(pos_sb[0][:], pos1)
+        load_w1(ww_late[1], slice(2, 4), slice(3 * P, H))
+        nc.sync.dma_start(pos_sb[1][:], pos2)
+        with nc.allow_non_contiguous_dma(reason="one weight a token and partition"):
+            for r in range(2):
+                nc.sync.dma_start(gate_col[r][:], gate[r, 0, P:].rearrange("(b p) -> p b", p=P))
 
         ident_raw = keep.tile([P, P], F32, name="ident_raw")
         ident = keep.tile([P, P], F32, name="ident")
         make_identity(nc, ident_raw[:])
-        load_w1_scales(1)
         nc.scalar.activation(ident[:], ident_raw[:], RELU)
 
-        for r in range(2):
-            spread = bank(6 + r)
-            for m in range(4):
-                nc.tensor.transpose(
-                    spread[:, m * P : (m + 1) * P], gate_row[:, r, m : m + 1].to_broadcast([P, P]), ident[:]
-                )
-            nc.scalar.copy(
-                gate_sb[:, r, :].rearrange("p (n m) -> p n m", m=4), spread[:].rearrange("p (m n) -> p n m", m=4)
-            )
+        h = [held(f"h{a}", [P, S], F32) for a in range(CHUNKS)]
+        gs = held("gs", [P, S], U8)
+        gw = [held(f"gw{s}", [P, S], U32) for s in range(PASSES)]
 
-        h = [keep.tile([P, S], F32, name=f"h{a}", align_bytes=64) for a in range(CHUNKS)]
-        gs = keep.tile([P, S], U8, name="gs", align_bytes=64)
-        gw = [keep.tile([P, S], U32, name=f"gw{s}", align_bytes=64) for s in range(PASSES)]
+        def gather_words(s, lo, hi):
+            window = xw[:, s * T :] if s or lo else xw[:, :T]
+            nc.vector.tensor_copy(gw[s][:, lo:hi], window.bitcast(U32).indirect(offs_sb[:, lo // 16 : hi // 16]))
 
-        def gather_words(s, lo, hi, window):
-            first = (1 - s) * T
-            nc.vector.tensor_copy(
-                gw[s][:, lo:hi], xw[:, first : first + window].bitcast(U32).indirect(offs_sb[:, lo // 16 : hi // 16])
-            )
-
-        def product(acc, col, a, s, lo, hi, start, stop):
+        def product(acc, a, s, lo, hi, start, stop):
             e = lo // C
-            byte0 = (PASSES * e + s) * H // 2 + a % 2 * P
-            words = ww_early[e // 2][:, PASSES * (e % 2) + s] if a < 2 else ww_late[:, PASSES * e + s]
+            level = 4 * (PASSES * (e % 2) + s)
+            words = ww[e][:, s, a * P : (a + 1) * P] if a < 3 else ww_late[e // 2][:, PASSES * (e % 2) + s]
             nc.tensor.matmul_mx(
-                out=acc[:, col : col + hi - lo],
-                lhsT=words[:, (a % 2) * P : (a % 2 + 1) * P].bitcast(FP8X4),
-                lhsT_scale=ws[a // 2][:, byte0 : byte0 + P],
+                out=acc,
+                lhsT=words.bitcast(FP8X4),
+                lhsT_scale=ws[e // 2][level:P, a * P : (a + 1) * P],
                 rhs=gw[s][:, lo:hi].bitcast(FP8X4),
                 rhs_scale=gs[X_LEVEL + 4 * s : P, lo:hi],
                 start=start,
                 stop=stop,
             )
 
-        acc = {}
+        def hidden(lo, hi, banks):
+            sums = [bank(n) for n in banks]
+            for s in range(PASSES):
+                for a, acc in enumerate(sums):
+                    product(acc[:, : hi - lo], a, s, lo, hi, s == 0, s == PASSES - 1)
+            for a, acc in enumerate(sums):
+                nc.scalar.activation(h[a][:, lo:hi], acc[:, : hi - lo], RELU)
 
-        def open_sums(a, lo, hi, n):
-            acc[a, lo] = bank(n)
-            for e0 in range(lo, hi, C):
-                product(acc[a, lo], e0 - lo, a, 0, e0, min(hi, e0 + C), e0 == lo, False)
+        def hidden_late(lo, n):
+            acc = bank(n)
+            for s in range(PASSES):
+                for e in range(2):
+                    product(acc[:, e * C : (e + 1) * C], 3, s, lo + e * C, lo + (e + 1) * C, s + e == 0, s + e == 2)
+            nc.scalar.activation(h[3][:, lo : lo + 2 * C], acc[:], RELU)
 
-        def close_sums(a, lo, hi):
-            for e0 in range(lo, hi, C):
-                product(acc[a, lo], e0 - lo, a, 1, e0, min(hi, e0 + C), False, e0 + C >= hi)
-            nc.scalar.activation(h[a][:, lo:hi], acc[a, lo][:, : hi - lo], RELU)
+        def expert(e):
+            gather_words(0, e * C, (e + 1) * C)
+            gather_words(1, e * C, (e + 1) * C)
+            hidden(e * C, (e + 1) * C, range(4 * (e % 2), 4 * (e % 2) + 3))
 
-        gather_words(0, 0, S, WORD_WINDOW)
-        for lo in (0, 2 * C):
-            nc.vector.tensor_copy(gs[:, lo : lo + 2 * C], xs[:].indirect(offs_sb[:, lo // 16 : (lo + 2 * C) // 16]))
-        pieces = [(0, 2 * C), (2 * C, 3 * C), (3 * C, 3 * C + P), (3 * C + P, S)]
-        halves = [(0, 2 * C), (2 * C, S)]
-        for lo, hi in pieces:
-            gather_words(1, lo, hi, HALF_WINDOW if hi - lo == 2 * C else T)
-        open_sums(0, *pieces[0], 0)
-        open_sums(1, *halves[0], 4)
-        for n in range(1, 4):
-            open_sums(0, *pieces[n], n)
-        open_sums(1, *halves[1], 5)
-        for lo, hi in pieces:
-            close_sums(0, lo, hi)
-        for lo, hi in halves:
-            close_sums(1, lo, hi)
-        for a, (lo, hi), n in ((2, halves[0], 6), (2, halves[1], 7), (3, halves[0], 0)):
-            open_sums(a, lo, hi, n)
-            close_sums(a, lo, hi)
+        for lo in (0, S // 2):
+            nc.vector.tensor_copy(gs[:, lo : lo + S // 2], xs[:].indirect(offs_sb[:, lo // 16 : (lo + S // 2) // 16]))
+        for e in range(E - 1):
+            expert(e)
+        gather_words(0, 3 * C, S)
+        gather_words(1, 3 * C, 3 * C + P)
+        gather_words(1, 3 * C + P, S)
+        hidden(3 * C, 3 * C + P, (4, 5, 6))
+        hidden(3 * C + P, S, (3, 7, 0))
 
-        w2_bf = keep.tile([P, N, 4], BF16, name="w2_bf", align_bytes=64)
-        w2_codes = keep.tile([P, N], U32, name="w2_codes", align_bytes=64)
-        w2_scales = keep.tile([P, N], U8, name="w2_scales", align_bytes=64)
+        w2_bf = held("w2_bf", [P, N, 4], BF16)
+        w2_codes = held("w2_codes", [P, N], U32)
+        w2_scales = held("w2_scales", [P, N], U8)
         nc.vector.tensor_copy(w2_bf[:], w2_raw[:].rearrange("p j n -> p n j"))
         nc.vector.quantize_mx(
             out=w2_codes[:].bitcast(FP8X4), scales=w2_scales[:], in_=w2_bf[:].rearrange("p n j -> p (n j)")
         )
 
-        ct = keep.tile([P, T // P * H], BF16, name="ct", align_bytes=64)
+        ct = held("ct", [P, T // P * H], BF16)
 
-        prods = [[keep.tile([P, T], F32, name=f"prod{n}_{r}", align_bytes=64) for r in range(2)] for n in range(3)]
-
-        def gated(a, t0, width, tiles, col):
+        def fetched(a, b0, blocks, gated, name):
+            t0, width = b0 * P, blocks * P
+            tiles = [held(f"{name}_{r}", [P, width], F32) for r in range(2)]
             for r in range(2):
-                nc.vector.tensor_tensor(
-                    tiles[r][:, col : col + width],
-                    h[a][:].indirect(pos_sb[r][:, t0 // 16 : (t0 + width) // 16]),
-                    gate_sb[:, r, t0 : t0 + width],
-                    MULT,
-                )
+                columns = h[a][:].indirect(pos_sb[r][:, t0 // 16 : (t0 + width) // 16])
+                if gated:
+                    nc.vector.tensor_tensor(tiles[r][:], columns, gate_sb[b0 // 2][:, r, b0 % 2 * P : b0 % 2 * P + width], MULT)
+                else:
+                    nc.scalar.activation(tiles[r][:], columns, COPY)
+            return tiles
 
-        def add_turned(sums, tiles, col, r, start, stop):
-            nc.tensor.matmul(
-                sums, lhsT=tiles[r][:, col : col + P], rhs=ident[:], start=start, stop=stop, is_transpose=True
-            )
-
-        def round_sums(a, t0, sums):
-            width = sums.shape[1]
-            blocks = ct[:, t0 // P * H : (t0 + width) // P * H].rearrange("t (b u p e) -> t b u p e", u=2, p=P, e=2)
-            nc.scalar.copy(
-                blocks[:, :, :, 32 * a : 32 * (a + 1), :], sums.rearrange("t (b p u e) -> t b u p e", p=32, u=2, e=2)
-            )
-
-        def combine(a, t0, width, tiles, col, sums):
-            gated(a, t0, width, tiles, col)
-            blocks = width // P
+        def add_gated(a, b0, sums):
+            blocks = sums.shape[1] // P
+            tiles = fetched(a, b0, blocks, True, f"gated{a}_{b0}")
             for r in range(2):
                 for b in range(blocks):
-                    add_turned(
-                        sums[:, b * P : (b + 1) * P], tiles, col + b * P, r, r + b == 0, r == 1 and b == blocks - 1
+                    nc.tensor.matmul(
+                        sums[:, b * P : (b + 1) * P],
+                        lhsT=tiles[r][:, b * P : (b + 1) * P],
+                        rhs=ident[:],
+                        start=r + b == 0,
+                        stop=r == 1 and b == blocks - 1,
+                        is_transpose=True,
                     )
-            round_sums(a, t0, sums)
 
-        def warmed(n):
-            spare = bank(n)
-            for s in range(PASSES):
-                nc.tensor.matmul_mx(
-                    out=spare[:],
-                    lhsT=ww_late[:, s, :P].bitcast(FP8X4),
-                    lhsT_scale=ws[1][:, s * H // 2 : s * H // 2 + P],
-                    rhs=gw[s][:, :BANK].bitcast(FP8X4),
-                    rhs_scale=gs[X_LEVEL + 4 * s : P, :BANK],
-                    start=(s == 0),
-                    stop=(s == PASSES - 1),
+        def round_sums(b0, blocks, a0, sums):
+            rows = sums.shape[1] // blocks // 4
+            nc.scalar.copy(
+                ct[:, b0 * H : (b0 + blocks) * H].rearrange("t (b u p e) -> t b u p e", u=2, p=P, e=2)[
+                    :, :, :, 32 * a0 : 32 * a0 + rows, :
+                ],
+                sums.rearrange("t (b p u e) -> t b u p e", p=rows, u=2, e=2),
+            )
+
+        def combine(a, b0, blocks, n):
+            sums = bank(n)[:, : blocks * P]
+            add_gated(a, b0, sums)
+            return sums
+
+        def turn_plain(a, tiles, col, both):
+            for r in range(2):
+                at = (2 * r + a % 2) * P
+                nc.tensor.transpose(both[:, at : at + P], tiles[r][:, col : col + P], ident[:])
+
+        def scale_on_scalar(dst, src, factor):
+            nc.scalar.activation(dst, src, COPY, scale=factor)
+
+        def scale_on_vector(dst, src, factor):
+            nc.vector.tensor_scalar(dst, src, factor, None, MULT)
+
+        def weigh(b, both, scale):
+            first = held(f"first{b}", [P, 2, P], F32)
+            scale(
+                first[:].rearrange("t u (p e) -> t u p e", e=2),
+                both[:, : 2 * P].rearrange("t (p u e) -> t u p e", u=2, e=2),
+                gate_col[0][:, b - 1 : b],
+            )
+            for u in range(2):
+                nc.vector.scalar_tensor_tensor(
+                    ct[:, b * H + u * 2 * P : b * H + u * 2 * P + P].rearrange("t (p e) -> t p e", e=2),
+                    both[:, 2 * P :].rearrange("t (p u e) -> t u p e", u=2, e=2)[:, u],
+                    gate_col[1][:, b - 1 : b],
+                    first[:, u, :].rearrange("t (p e) -> t p e", e=2),
+                    MULT,
+                    ADD,
                 )
-            return spare
 
-        def turn_back(g):
-            t0, width = GROUPS[g]
-            back = bank((1, 3, 7)[g])
-            for b in range(width // P):
-                words = ct[:, (t0 // P + b) * H : (t0 // P + b + 1) * H].bitcast(F32)
+        res = held("res", [P, T], F32)
+
+        def turn_back(b0, blocks, n):
+            back = bank(n)
+            width = blocks * P
+            for b in range(blocks):
+                words = ct[:, (b0 + b) * H : (b0 + b + 1) * H].bitcast(F32)
                 for u in range(2):
                     nc.tensor.transpose(
                         back[:, u * width + b * P : u * width + (b + 1) * P], words[:, u * P : (u + 1) * P], ident[:]
                     )
-            parts = []
-            for p0, n in PARTS:
-                if t0 <= p0 < t0 + width:
-                    c_bf = keep.tile([P, n * 4], BF16, name=f"c_bf{p0}", align_bytes=64)
-                    (nc.vector.tensor_copy if g < 2 else nc.scalar.copy)(
-                        c_bf[:].bitcast(F32).rearrange("p (t u) -> p t u", u=2),
-                        back[:, : 2 * width].rearrange("p (u t) -> p t u", u=2)[:, p0 - t0 : p0 - t0 + n, :],
-                    )
-                    parts.append(c_bf)
-            return parts
+            return back[:, : 2 * width].rearrange("p (u t) -> p t u", u=2)
 
-        res = keep.tile([P, T], F32, name="res", align_bytes=64)
-
-        def project(g, c_bf):
-            t0, width = PARTS[g]
-            codes = keep.tile([P, width], U32, name=f"c_codes{g}", align_bytes=64)
-            scales = keep.tile([P, width], U8, name=f"c_scales{g}", align_bytes=64)
+        def project(t0, pairs, n, copy_words, copy_result):
+            width = pairs.shape[1]
+            c_bf = held(f"c_bf{t0}", [P, width * 4], BF16)
+            codes = held(f"c_codes{t0}", [P, width], U32)
+            scales = held(f"c_scales{t0}", [P, width], U8)
+            copy_words(c_bf[:].bitcast(F32).rearrange("p (t u) -> p t u", u=2), pairs)
             nc.vector.quantize_mx(out=codes[:].bitcast(FP8X4), scales=scales[:], in_=c_bf[:])
-            proj = bank((2, 4, 5, 0)[g])
+            proj = bank(n)
             nc.tensor.matmul_mx(
                 out=proj[:, :width],
                 lhsT=w2_codes[:].bitcast(FP8X4),
@@ -257,39 +264,36 @@ def tile_moe_sdn_lin_relu_kernel(
                 start=True,
                 stop=True,
             )
-            if g == 0:
-                nc.scalar.copy(res[:, t0 : t0 + width], proj[:, :width])
-            else:
-                nc.vector.tensor_copy(res[:, t0 : t0 + width], proj[:, :width])
-            for first, n in GROUPS:
-                if first + n == t0 + width:
-                    nc.sync.dma_start(out[:, first : first + n], res[:, first : first + n])
+            copy_result(res[:, t0 : t0 + width], proj[:, :width])
 
-        gated(0, 0, T, prods[0], 0)
-        opening = [bank(6), bank(7)]
-        for r in range(2):
-            for b in range(4):
-                add_turned(
-                    opening[b // 2][:, b % 2 * P : (b % 2 + 1) * P], prods[0], b * P, r, r + b % 2 == 0, r + b % 2 == 2
-                )
-        for n in range(2):
-            round_sums(0, n * HALF, opening[n][:, :HALF])
-        open_sums(3, *halves[1], 6)
-        close_sums(3, *halves[1])
-        combine(1, 0, T, prods[1], 0, bank(7)[:])
-        combine(2, 0, HALF, prods[2], 0, warmed(6)[:, :HALF])
-        gated(3, 0, HALF, prods[2], HALF)
-        closing = [bank(7), bank(2)]
-        for r in range(2):
-            for b in range(2):
-                add_turned(closing[b][:, :P], prods[2], HALF + b * P, r, r == 0, r == 1)
-        for b in range(2):
-            round_sums(3, b * P, closing[b][:, :P])
-        rounded = turn_back(0)
-        combine(2, HALF, HALF, prods[1], 0, warmed(6)[:, :HALF])
-        combine(3, HALF, P, prods[1], HALF, bank(7)[:, :P])
-        combine(3, HALF + P, P, prods[1], HALF + P, bank(2)[:, :P])
-        for g in (1, 2):
-            rounded.extend(turn_back(g))
-        for g in range(len(PARTS)):
-            project(g, rounded[g])
+        def store(t0, width):
+            nc.sync.dma_start(out[:, t0 : t0 + width], res[:, t0 : t0 + width])
+
+        hidden_late(0, 1)
+        hidden_late(2 * C, 2)
+        low = [bank(n) for n in (4, 5, 6, 3)]
+        for a in range(2):
+            add_gated(a, 0, low[0][:, a * P : (a + 1) * P])
+        for a in range(2):
+            turn_plain(a, fetched(a, 1, 1, False, f"plain{a}_1"), 0, low[1])
+        third = [combine(2, 0, 2, 0), combine(2, 2, 2, 7)]
+        for a in range(2):
+            plain = fetched(a, 2, 2, False, f"plain{a}_2")
+            for b in (2, 3):
+                turn_plain(a, plain, (b - 2) * P, low[b])
+        fourth = [combine(3, 0, 2, 1), combine(3, 2, 2, 2)]
+        round_sums(0, 1, 0, low[0][:, : 2 * P])
+        round_sums(0, 2, 2, third[0])
+        weigh(1, low[1], scale_on_scalar)
+        round_sums(0, 2, 3, fourth[0])
+        pairs0 = turn_back(0, 2, 4)
+        weigh(3, low[3], scale_on_vector)
+        round_sums(2, 2, 2, third[1])
+        weigh(2, low[2], scale_on_scalar)
+        round_sums(2, 2, 3, fourth[1])
+        pairs2 = turn_back(2, 2, 0)
+        project(0, pairs0, 5, nc.scalar.copy, nc.scalar.copy)
+        store(0, 2 * P)
+        project(2 * P, pairs2[:, :P], 1, nc.vector.tensor_copy, nc.vector.tensor_copy)
+        project(3 * P, pairs2[:, P:], 7, nc.scalar.copy, nc.vector.tensor_copy)
+        store(2 * P, 2 * P)

@@ -54,9 +54,9 @@ def tile_moe_sdn_lin_relu_kernel(
         gate_col = [held(f"gate_col{r}", [P, 3], F32) for r in range(2)]
         w2_raw = held("w2_raw", [P, 4, N], F32)
 
-        nc.gpsimd.memset(xs[:].bitcast(I32), 0)
+        nc.vector.memset(xs[:].bitcast(I32), 0)
         for pair in range(2):
-            nc.gpsimd.memset(ws[pair][:].bitcast(I32), 0)
+            nc.vector.memset(ws[pair][:].bitcast(I32), 0)
 
         def load_x_words(s):
             nc.sync.dma_start(xw[:, s * T : (s + 1) * T], x_words[s].rearrange("p t d -> p (t d)").bitcast(I32))
@@ -75,13 +75,13 @@ def tile_moe_sdn_lin_relu_kernel(
             cols = slice(half * T // 2, (half + 1) * T // 2)
             nc.sync.dma_start(gate_sb[half][:], gate[:, :, cols].rearrange("r p t -> p r t"))
 
+        load_x_words(0)
+        nc.sync.dma_start(offs_sb[:], offs)
         for q in range(4):
             nc.sync.dma_start(
                 xs[32 * q + X_LEVEL : 32 * q + X_LEVEL + 8, :T].bitcast(I32),
                 x_scales[:, 4 * q : 4 * q + 4, :].bitcast(I32),
             )
-        nc.sync.dma_start(offs_sb[:], offs)
-        load_x_words(0)
         load_x_words(1)
         load_w1(ww[0], slice(0, 1), slice(0, 3 * P))
         load_w1_scales(0)
@@ -92,25 +92,23 @@ def tile_moe_sdn_lin_relu_kernel(
         load_w1(ww_late[0], slice(0, 2), slice(3 * P, H))
         nc.sync.dma_start(w2_raw[:], w2.rearrange("(p j) n -> p j n", j=4))
         load_gate(0)
-        load_gate(1)
         nc.sync.dma_start(pos_sb[0][:], pos1)
         load_w1(ww_late[1], slice(2, 4), slice(3 * P, H))
         nc.sync.dma_start(pos_sb[1][:], pos2)
+        load_gate(1)
         with nc.allow_non_contiguous_dma(reason="one weight a token and partition"):
             for r in range(2):
                 nc.sync.dma_start(gate_col[r][:], gate[r, 0, P:].rearrange("(b p) -> p b", p=P))
 
-        ident_raw = keep.tile([P, P], F32, name="ident_raw")
         ident = keep.tile([P, P], F32, name="ident")
-        make_identity(nc, ident_raw[:])
-        nc.scalar.activation(ident[:], ident_raw[:], RELU)
+        make_identity(nc, ident[:])
 
         h = [held(f"h{a}", [P, S], F32) for a in range(CHUNKS)]
         gs = held("gs", [P, S], U8)
         gw = [held(f"gw{s}", [P, S], U32) for s in range(PASSES)]
 
         def gather_words(s, lo, hi):
-            window = xw[:, s * T :] if s or lo else xw[:, :T]
+            window = xw[:, s * T :] if s or lo >= 2 * C else xw[:, :T]
             nc.vector.tensor_copy(gw[s][:, lo:hi], window.bitcast(U32).indirect(offs_sb[:, lo // 16 : hi // 16]))
 
         def product(acc, a, s, lo, hi, start, stop):
@@ -127,13 +125,16 @@ def tile_moe_sdn_lin_relu_kernel(
                 stop=stop,
             )
 
-        def hidden(lo, hi, banks):
+        def sums_early(lo, hi, banks):
             sums = [bank(n) for n in banks]
             for s in range(PASSES):
                 for a, acc in enumerate(sums):
                     product(acc[:, : hi - lo], a, s, lo, hi, s == 0, s == PASSES - 1)
-            for a, acc in enumerate(sums):
-                nc.scalar.activation(h[a][:, lo:hi], acc[:, : hi - lo], RELU)
+            return sums
+
+        def rectify(lo, hi, sums, chunks):
+            for a in chunks:
+                nc.scalar.activation(h[a][:, lo:hi], sums[a][:, : hi - lo], RELU)
 
         def hidden_late(lo, n):
             acc = bank(n)
@@ -142,20 +143,29 @@ def tile_moe_sdn_lin_relu_kernel(
                     product(acc[:, e * C : (e + 1) * C], 3, s, lo + e * C, lo + (e + 1) * C, s + e == 0, s + e == 2)
             nc.scalar.activation(h[3][:, lo : lo + 2 * C], acc[:], RELU)
 
-        def expert(e):
-            gather_words(0, e * C, (e + 1) * C)
-            gather_words(1, e * C, (e + 1) * C)
-            hidden(e * C, (e + 1) * C, range(4 * (e % 2), 4 * (e % 2) + 3))
+        def gather_scales(lo, hi):
+            nc.vector.tensor_copy(gs[:, lo:hi], xs[:].indirect(offs_sb[:, lo // 16 : hi // 16]))
 
-        for lo in (0, S // 2):
-            nc.vector.tensor_copy(gs[:, lo : lo + S // 2], xs[:].indirect(offs_sb[:, lo // 16 : (lo + S // 2) // 16]))
-        for e in range(E - 1):
-            expert(e)
+        for e in range(2):
+            gather_words(0, e * C, (e + 1) * C)
+        for half in range(2):
+            gather_scales(half * 2 * C, (half + 1) * 2 * C)
+        for e in range(2):
+            gather_words(1, e * C, (e + 1) * C)
+            rectify(e * C, (e + 1) * C, sums_early(e * C, (e + 1) * C, range(4 * e, 4 * e + 3)), range(3))
+        pieces = ((2 * C, 3 * C, (0, 1, 2)), (3 * C, 3 * C + P, (4, 5, 6)), (3 * C + P, S, (3, 7, 0)))
+        for s in range(PASSES):
+            gather_words(s, 2 * C, 3 * C)
         gather_words(0, 3 * C, S)
-        gather_words(1, 3 * C, 3 * C + P)
-        gather_words(1, 3 * C + P, S)
-        hidden(3 * C, 3 * C + P, (4, 5, 6))
-        hidden(3 * C + P, S, (3, 7, 0))
+        for lo, hi, banks in pieces[1:]:
+            gather_words(1, lo, hi)
+        sums = []
+        for lo, hi, banks in pieces:
+            sums.append(sums_early(lo, hi, banks))
+            rectify(lo, hi, sums[-1], (0,))
+        for a in (1, 2):
+            for (lo, hi, banks), acc in zip(pieces, sums):
+                rectify(lo, hi, acc, (a,))
 
         w2_bf = held("w2_bf", [P, N, 4], BF16)
         w2_codes = held("w2_codes", [P, N], U32)
@@ -274,26 +284,33 @@ def tile_moe_sdn_lin_relu_kernel(
         low = [bank(n) for n in (4, 5, 6, 3)]
         for a in range(2):
             add_gated(a, 0, low[0][:, a * P : (a + 1) * P])
+        third = [combine(2, 0, 2, 0)]
         for a in range(2):
             turn_plain(a, fetched(a, 1, 1, False, f"plain{a}_1"), 0, low[1])
-        third = [combine(2, 0, 2, 0), combine(2, 2, 2, 7)]
-        for a in range(2):
-            plain = fetched(a, 2, 2, False, f"plain{a}_2")
-            for b in (2, 3):
-                turn_plain(a, plain, (b - 2) * P, low[b])
-        fourth = [combine(3, 0, 2, 1), combine(3, 2, 2, 2)]
+        third.append(combine(2, 2, 2, 7))
+        plain = fetched(0, 2, 2, False, "plain0_2")
+        for b in (2, 3):
+            turn_plain(0, plain, (b - 2) * P, low[b])
+        fourth = combine(3, 0, 2, 1)
+        plain = fetched(1, 2, 2, False, "plain1_2")
+        for b in (2, 3):
+            turn_plain(1, plain, (b - 2) * P, low[b])
         round_sums(0, 1, 0, low[0][:, : 2 * P])
-        round_sums(0, 2, 2, third[0])
+        last = [combine(3, 2, 1, 2), combine(3, 3, 1, 4)]
         weigh(1, low[1], scale_on_scalar)
-        round_sums(0, 2, 3, fourth[0])
-        pairs0 = turn_back(0, 2, 4)
-        weigh(3, low[3], scale_on_vector)
-        round_sums(2, 2, 2, third[1])
+        round_sums(0, 2, 2, third[0])
         weigh(2, low[2], scale_on_scalar)
-        round_sums(2, 2, 3, fourth[1])
-        pairs2 = turn_back(2, 2, 0)
-        project(0, pairs0, 5, nc.scalar.copy, nc.scalar.copy)
+        round_sums(0, 2, 3, fourth)
+        pairs0 = turn_back(0, 2, 0)
+        round_sums(2, 2, 2, third[1])
+        round_sums(2, 1, 3, last[0])
+        pairs2 = turn_back(2, 1, 5)
+        weigh(3, low[3], scale_on_scalar)
+        round_sums(3, 1, 3, last[1])
+        pairs3 = turn_back(3, 1, 7)
+        project(0, pairs0, 1, nc.scalar.copy, nc.scalar.copy)
         store(0, 2 * P)
-        project(2 * P, pairs2[:, :P], 1, nc.vector.tensor_copy, nc.vector.tensor_copy)
-        project(3 * P, pairs2[:, P:], 7, nc.scalar.copy, nc.vector.tensor_copy)
-        store(2 * P, 2 * P)
+        project(2 * P, pairs2, 2, nc.vector.tensor_copy, nc.vector.tensor_copy)
+        store(2 * P, P)
+        project(3 * P, pairs3, 4, nc.scalar.copy, nc.scalar.copy)
+        store(3 * P, P)

@@ -281,6 +281,17 @@ def tile_moe_sdn_lin_relu_kernel(
 
         hidden_late(0, 1)
         hidden_late(2 * C, 2)
+        spare = bank(2)
+        for s in range(PASSES):
+            nc.tensor.matmul_mx(
+                out=spare[:],
+                lhsT=ww_late[0][:, s].bitcast(FP8X4),
+                lhsT_scale=ws[0][:, :P],
+                rhs=ww_late[1][:].rearrange("p g i -> p (g i)").bitcast(FP8X4),
+                rhs_scale=ws[1][:],
+                start=(s == 0),
+                stop=(s == PASSES - 1),
+            )
         low = [bank(n) for n in (4, 5, 6, 3)]
         for a in range(2):
             add_gated(a, 0, low[0][:, a * P : (a + 1) * P])

@@ -48,7 +48,8 @@ def tile_moe_sdn_lin_relu_kernel(
         xs = held("xs", [P, BYTE_WINDOW], U8)
         xw = held("xw", [P, PASSES * T], I32)
         ws = [held(f"ws{pair}", [P, H], U8) for pair in range(2)]
-        ww = [held(f"ww{e}", [P, PASSES, 3 * P], I32) for e in range(E)]
+        ww_first = held("ww_first", [P, 2 * PASSES, 3 * P], I32)
+        ww = [held(f"ww{e}", [P, PASSES, 3 * P], I32) for e in range(2)]
         ww_late = [held(f"ww_late{pair}", [P, 2 * PASSES, P], I32) for pair in range(2)]
         gate_sb = [held(f"gate_sb{half}", [P, 2, T // 2], F32) for half in range(2)]
         gate_col = [held(f"gate_col{r}", [P, 3], F32) for r in range(2)]
@@ -83,19 +84,18 @@ def tile_moe_sdn_lin_relu_kernel(
                 x_scales[:, 4 * q : 4 * q + 4, :].bitcast(I32),
             )
         load_x_words(1)
-        load_w1(ww[0], slice(0, 1), slice(0, 3 * P))
+        load_w1(ww_first, slice(0, 2), slice(0, 3 * P))
         load_w1_scales(0)
-        load_w1(ww[1], slice(1, 2), slice(0, 3 * P))
-        load_w1(ww[2], slice(2, 3), slice(0, 3 * P))
+        load_w1(ww[0], slice(2, 3), slice(0, 3 * P))
         load_w1_scales(1)
-        load_w1(ww[3], slice(3, 4), slice(0, 3 * P))
+        load_w1(ww[1], slice(3, 4), slice(0, 3 * P))
         load_w1(ww_late[0], slice(0, 2), slice(3 * P, H))
         nc.sync.dma_start(w2_raw[:], w2.rearrange("(p j) n -> p j n", j=4))
         load_gate(0)
         nc.sync.dma_start(pos_sb[0][:], pos1)
         load_w1(ww_late[1], slice(2, 4), slice(3 * P, H))
-        nc.sync.dma_start(pos_sb[1][:], pos2)
         load_gate(1)
+        nc.sync.dma_start(pos_sb[1][:], pos2)
         with nc.allow_non_contiguous_dma(reason="one weight a token and partition"):
             for r in range(2):
                 nc.sync.dma_start(gate_col[r][:], gate[r, 0, P:].rearrange("(b p) -> p b", p=P))
@@ -114,7 +114,8 @@ def tile_moe_sdn_lin_relu_kernel(
         def product(acc, a, s, lo, hi, start, stop):
             e = lo // C
             level = 4 * (PASSES * (e % 2) + s)
-            words = ww[e][:, s, a * P : (a + 1) * P] if a < 3 else ww_late[e // 2][:, PASSES * (e % 2) + s]
+            early = ww_first[:, PASSES * e + s] if e < 2 else ww[e - 2][:, s]
+            words = early[:, a * P : (a + 1) * P] if a < 3 else ww_late[e // 2][:, PASSES * (e % 2) + s]
             nc.tensor.matmul_mx(
                 out=acc,
                 lhsT=words.bitcast(FP8X4),
@@ -125,16 +126,13 @@ def tile_moe_sdn_lin_relu_kernel(
                 stop=stop,
             )
 
-        def sums_early(lo, hi, banks):
-            sums = [bank(n) for n in banks]
+        def hidden(pieces):
+            sums = [bank(n)[:, : hi - lo] for a, lo, hi, n in pieces]
             for s in range(PASSES):
-                for a, acc in enumerate(sums):
-                    product(acc[:, : hi - lo], a, s, lo, hi, s == 0, s == PASSES - 1)
-            return sums
-
-        def rectify(lo, hi, sums, chunks):
-            for a in chunks:
-                nc.scalar.activation(h[a][:, lo:hi], sums[a][:, : hi - lo], RELU)
+                for (a, lo, hi, n), acc in zip(pieces, sums):
+                    product(acc, a, s, lo, hi, s == 0, s == PASSES - 1)
+            for (a, lo, hi, n), acc in zip(pieces, sums):
+                nc.scalar.activation(h[a][:, lo:hi], acc, RELU)
 
         def hidden_late(lo, n):
             acc = bank(n)
@@ -152,20 +150,14 @@ def tile_moe_sdn_lin_relu_kernel(
             gather_scales(half * 2 * C, (half + 1) * 2 * C)
         for e in range(2):
             gather_words(1, e * C, (e + 1) * C)
-            rectify(e * C, (e + 1) * C, sums_early(e * C, (e + 1) * C, range(4 * e, 4 * e + 3)), range(3))
-        pieces = ((2 * C, 3 * C, (0, 1, 2)), (3 * C, 3 * C + P, (4, 5, 6)), (3 * C + P, S, (3, 7, 0)))
+        hidden([(a, e * C, (e + 1) * C, 4 * e + a) for e in range(2) for a in range(3)])
         for s in range(PASSES):
             gather_words(s, 2 * C, 3 * C)
+        hidden([(a, 2 * C, 3 * C, a) for a in range(3)])
         gather_words(0, 3 * C, S)
-        for lo, hi, banks in pieces[1:]:
-            gather_words(1, lo, hi)
-        sums = []
-        for lo, hi, banks in pieces:
-            sums.append(sums_early(lo, hi, banks))
-            rectify(lo, hi, sums[-1], (0,))
-        for a in (1, 2):
-            for (lo, hi, banks), acc in zip(pieces, sums):
-                rectify(lo, hi, acc, (a,))
+        gather_words(1, 3 * C, 3 * C + P)
+        gather_words(1, 3 * C + P, S)
+        hidden([(0, 3 * C, 3 * C + P, 3), (0, 3 * C + P, S, 7), (1, 3 * C, S, 4), (2, 3 * C, S, 5)])
 
         w2_bf = held("w2_bf", [P, N, 4], BF16)
         w2_codes = held("w2_codes", [P, N], U32)
@@ -175,7 +167,10 @@ def tile_moe_sdn_lin_relu_kernel(
             out=w2_codes[:].bitcast(FP8X4), scales=w2_scales[:], in_=w2_bf[:].rearrange("p n j -> p (n j)")
         )
 
-        ct = held("ct", [P, T // P * H], BF16)
+        ct = [held(f"ct{half}", [P, 2 * H], BF16) for half in range(2)]
+
+        def rounded(b0, blocks):
+            return ct[b0 // 2][:, b0 % 2 * H : (b0 % 2 + blocks) * H]
 
         def fetched(a, b0, blocks, gated, name):
             t0, width = b0 * P, blocks * P
@@ -205,7 +200,7 @@ def tile_moe_sdn_lin_relu_kernel(
         def round_sums(b0, blocks, a0, sums):
             rows = sums.shape[1] // blocks // 4
             nc.scalar.copy(
-                ct[:, b0 * H : (b0 + blocks) * H].rearrange("t (b u p e) -> t b u p e", u=2, p=P, e=2)[
+                rounded(b0, blocks).rearrange("t (b u p e) -> t b u p e", u=2, p=P, e=2)[
                     :, :, :, 32 * a0 : 32 * a0 + rows, :
                 ],
                 sums.rearrange("t (b p u e) -> t b u p e", p=rows, u=2, e=2),
@@ -236,7 +231,7 @@ def tile_moe_sdn_lin_relu_kernel(
             )
             for u in range(2):
                 nc.vector.scalar_tensor_tensor(
-                    ct[:, b * H + u * 2 * P : b * H + u * 2 * P + P].rearrange("t (p e) -> t p e", e=2),
+                    rounded(b, 1)[:, u * 2 * P : u * 2 * P + P].rearrange("t (p e) -> t p e", e=2),
                     both[:, 2 * P :].rearrange("t (p u e) -> t u p e", u=2, e=2)[:, u],
                     gate_col[1][:, b - 1 : b],
                     first[:, u, :].rearrange("t (p e) -> t p e", e=2),
@@ -250,20 +245,22 @@ def tile_moe_sdn_lin_relu_kernel(
             back = bank(n)
             width = blocks * P
             for b in range(blocks):
-                words = ct[:, (b0 + b) * H : (b0 + b + 1) * H].bitcast(F32)
+                words = rounded(b0 + b, 1).bitcast(F32)
                 for u in range(2):
                     nc.tensor.transpose(
                         back[:, u * width + b * P : u * width + (b + 1) * P], words[:, u * P : (u + 1) * P], ident[:]
                     )
             return back[:, : 2 * width].rearrange("p (u t) -> p t u", u=2)
 
-        def project(t0, pairs, n, copy_words, copy_result):
-            width = pairs.shape[1]
-            c_bf = held(f"c_bf{t0}", [P, width * 4], BF16)
+        c_bf = held("c_bf", [P, T * 4], BF16)
+
+        def lay_out(b, n, copy):
+            copy(c_bf[:, b * BANK : (b + 1) * BANK].bitcast(F32).rearrange("p (t u) -> p t u", u=2), turn_back(b, 1, n))
+
+        def project(t0, width, n, copy_result):
             codes = held(f"c_codes{t0}", [P, width], U32)
             scales = held(f"c_scales{t0}", [P, width], U8)
-            copy_words(c_bf[:].bitcast(F32).rearrange("p (t u) -> p t u", u=2), pairs)
-            nc.vector.quantize_mx(out=codes[:].bitcast(FP8X4), scales=scales[:], in_=c_bf[:])
+            nc.vector.quantize_mx(out=codes[:].bitcast(FP8X4), scales=scales[:], in_=c_bf[:, 4 * t0 : 4 * (t0 + width)])
             proj = bank(n)
             nc.tensor.matmul_mx(
                 out=proj[:, :width],
@@ -308,20 +305,22 @@ def tile_moe_sdn_lin_relu_kernel(
             turn_plain(1, plain, (b - 2) * P, low[b])
         round_sums(0, 1, 0, low[0][:, : 2 * P])
         last = [combine(3, 2, 1, 2), combine(3, 3, 1, 4)]
-        weigh(1, low[1], scale_on_scalar)
         round_sums(0, 2, 2, third[0])
-        weigh(2, low[2], scale_on_scalar)
         round_sums(0, 2, 3, fourth)
-        pairs0 = turn_back(0, 2, 0)
+        first_pairs = turn_back(0, 1, 0)
+        weigh(1, low[1], scale_on_scalar)
+        weigh(2, low[2], scale_on_scalar)
+        nc.vector.tensor_copy(c_bf[:, :BANK].bitcast(F32).rearrange("p (t u) -> p t u", u=2), first_pairs)
         round_sums(2, 2, 2, third[1])
-        round_sums(2, 1, 3, last[0])
-        pairs2 = turn_back(2, 1, 5)
         weigh(3, low[3], scale_on_scalar)
+        round_sums(2, 1, 3, last[0])
         round_sums(3, 1, 3, last[1])
-        pairs3 = turn_back(3, 1, 7)
-        project(0, pairs0, 1, nc.scalar.copy, nc.scalar.copy)
+        lay_out(1, 1, nc.scalar.copy)
+        project(0, 2 * P, 2, nc.scalar.copy)
         store(0, 2 * P)
-        project(2 * P, pairs2, 2, nc.vector.tensor_copy, nc.vector.tensor_copy)
+        lay_out(2, 5, nc.vector.tensor_copy)
+        project(2 * P, P, 6, nc.vector.tensor_copy)
         store(2 * P, P)
-        project(3 * P, pairs3, 4, nc.scalar.copy, nc.scalar.copy)
+        lay_out(3, 7, nc.scalar.copy)
+        project(3 * P, P, 3, nc.scalar.copy)
         store(3 * P, P)

@@ -83,9 +83,9 @@ def tile_moe_sdn_lin_relu_kernel(
                 xs[32 * q + X_LEVEL : 32 * q + X_LEVEL + 8, :T].bitcast(I32),
                 x_scales[:, 4 * q : 4 * q + 4, :].bitcast(I32),
             )
-        load_x_words(1)
         load_w1(ww_first, slice(0, 2), slice(0, 3 * P))
         load_w1_scales(0)
+        load_x_words(1)
         load_w1(ww[0], slice(2, 3), slice(0, 3 * P))
         load_w1_scales(1)
         load_w1(ww[1], slice(3, 4), slice(0, 3 * P))

@@ -278,17 +278,6 @@ def tile_moe_sdn_lin_relu_kernel(
 
         hidden_late(0, 1)
         hidden_late(2 * C, 2)
-        spare = bank(2)
-        for s in range(PASSES):
-            nc.tensor.matmul_mx(
-                out=spare[:],
-                lhsT=ww_late[0][:, s].bitcast(FP8X4),
-                lhsT_scale=ws[0][:, :P],
-                rhs=ww_late[1][:].rearrange("p g i -> p (g i)").bitcast(FP8X4),
-                rhs_scale=ws[1][:],
-                start=(s == 0),
-                stop=(s == PASSES - 1),
-            )
         low = [bank(n) for n in (4, 5, 6, 3)]
         for a in range(2):
             add_gated(a, 0, low[0][:, a * P : (a + 1) * P])

from contextlib import ExitStack

import concourse.mybir as mybir
from concourse.masks import make_identity

K, T, E, C, H, N = 1024, 512, 4, 256, 512, 128
S = E * C
FLOPS = 2 * K * H * S + 2 * H * N * T

F32 = mybir.dt.float32
BF16 = mybir.dt.bfloat16
I32 = mybir.dt.int32
U32 = mybir.dt.uint32
U16 = mybir.dt.uint16
U8 = mybir.dt.uint8
FP8X4 = mybir.dt.float8_e4m3fn_x4
RELU = mybir.ActivationFunctionType.Relu
COPY = mybir.ActivationFunctionType.Copy
MULT = mybir.AluOpType.mult
ADD = mybir.AluOpType.add

P = 128
PASSES = K // 512
CHUNKS = H // P
BANK = 512
X_LEVEL = 8
BYTE_WINDOW = 704


def tile_moe_sdn_lin_relu_kernel(
    tc, x_words, x_scales, w1_words, w1_scales, w2, gate, offs, pos1, pos2, out
):
    nc = tc.nc
    with ExitStack() as ctx:
        lists = ctx.enter_context(tc.tile_pool(name="lists", bufs=1))
        keep = ctx.enter_context(tc.tile_pool(name="keep", bufs=1))
        psum = ctx.enter_context(tc.psum_pool(name="psum", bufs=1))

        def bank(n):
            return psum.tile([P, BANK], F32, name=f"bank{n}")

        def held(name, shape, dtype):
            return keep.tile(shape, dtype, name=name, align_bytes=64)

        offs_sb = lists.tile([P, S // 16], U16, name="offs_sb")
        pos_sb = [lists.tile([P, T // 16], U16, name=f"pos_sb{r}") for r in range(2)]

        xs = held("xs", [P, BYTE_WINDOW], U8)
        xw = held("xw", [P, PASSES * T], I32)
        ws = [held(f"ws{pair}", [P, H], U8) for pair in range(2)]
        ww_first = held("ww_first", [P, 2 * PASSES, 3 * P], I32)
        ww = [held(f"ww{e}", [P, PASSES, 3 * P], I32) for e in range(2)]
        ww_late = [held(f"ww_late{pair}", [P, 2 * PASSES, P], I32) for pair in range(2)]
        gate_sb = [held(f"gate_sb{half}", [P, 2, T // 2], F32) for half in range(2)]
        gate_col = [held(f"gate_col{r}", [P, 3], F32) for r in range(2)]
        w2_raw = held("w2_raw", [P, 4, N], F32)

        nc.vector.memset(xs[:].bitcast(I32), 0)
        for pair in range(2):
            nc.vector.memset(ws[pair][:].bitcast(I32), 0)

        def load_x_words(s):
            nc.sync.dma_start(xw[:, s * T : (s + 1) * T], x_words[s].rearrange("p t d -> p (t d)").bitcast(I32))

        def load_w1(tile, experts, cols):
            nc.sync.dma_start(
                tile[:], w1_words[experts, :, :, cols, :].rearrange("e s p i d -> p (e s) (i d)").bitcast(I32)
            )

        def load_w1_scales(pair):
            rows = w1_scales.rearrange("(c h) s (q r) i -> c q (h s) r i", h=2, r=4).bitcast(I32)
            for q in range(4):
                nc.sync.dma_start(ws[pair][32 * q : 32 * q + 16, :].bitcast(I32), rows[pair, q])

        def load_gate(half):
            cols = slice(half * T // 2, (half + 1) * T // 2)
            nc.sync.dma_start(gate_sb[half][:], gate[:, :, cols].rearrange("r p t -> p r t"))

        load_x_words(0)
        nc.sync.dma_start(offs_sb[:], offs)
        for q in range(4):
            nc.sync.dma_start(
                xs[32 * q + X_LEVEL : 32 * q + X_LEVEL + 8, :T].bitcast(I32),
                x_scales[:, 4 * q : 4 * q + 4, :].bitcast(I32),
            )
        load_w1(ww_first, slice(0, 2), slice(0, 3 * P))
        load_w1_scales(0)
        load_x_words(1)
        load_w1(ww[0], slice(2, 3), slice(0, 3 * P))
        load_w1_scales(1)
        load_w1(ww[1], slice(3, 4), slice(0, 3 * P))
        load_w1(ww_late[0], slice(0, 2), slice(3 * P, H))
        nc.sync.dma_start(w2_raw[:], w2.rearrange("(p j) n -> p j n", j=4))
        load_gate(0)
        nc.sync.dma_start(pos_sb[0][:], pos1)
        load_w1(ww_late[1], slice(2, 4), slice(3 * P, H))
        load_gate(1)
        nc.sync.dma_start(pos_sb[1][:], pos2)
        with nc.allow_non_contiguous_dma(reason="one weight a token and partition"):
            for r in range(2):
                nc.sync.dma_start(gate_col[r][:], gate[r, 0, P:].rearrange("(b p) -> p b", p=P))

        ident = keep.tile([P, P], F32, name="ident")
        make_identity(nc, ident[:])

        h = [held(f"h{a}", [P, S], F32) for a in range(CHUNKS)]
        gs = held("gs", [P, S], U8)
        gw = [held(f"gw{s}", [P, S], U32) for s in range(PASSES)]

        def gather_words(s, lo, hi):
            window = xw[:, s * T :] if s or lo >= 2 * C else xw[:, :T]
            nc.vector.tensor_copy(gw[s][:, lo:hi], window.bitcast(U32).indirect(offs_sb[:, lo // 16 : hi // 16]))

        def product(acc, a, s, lo, hi, start, stop):
            e = lo // C
            level = 4 * (PASSES * (e % 2) + s)
            early = ww_first[:, PASSES * e + s] if e < 2 else ww[e - 2][:, s]
            words = early[:, a * P : (a + 1) * P] if a < 3 else ww_late[e // 2][:, PASSES * (e % 2) + s]
            nc.tensor.matmul_mx(
                out=acc,
                lhsT=words.bitcast(FP8X4),
                lhsT_scale=ws[e // 2][level:P, a * P : (a + 1) * P],
                rhs=gw[s][:, lo:hi].bitcast(FP8X4),
                rhs_scale=gs[X_LEVEL + 4 * s : P, lo:hi],
                start=start,
                stop=stop,
            )

        def hidden(pieces):
            sums = [bank(n)[:, : hi - lo] for a, lo, hi, n in pieces]
            for s in range(PASSES):
                for (a, lo, hi, n), acc in zip(pieces, sums):
                    product(acc, a, s, lo, hi, s == 0, s == PASSES - 1)
            for (a, lo, hi, n), acc in zip(pieces, sums):
                nc.scalar.activation(h[a][:, lo:hi], acc, RELU)

        def hidden_late(lo, n):
            acc = bank(n)
            for s in range(PASSES):
                for e in range(2):
                    product(acc[:, e * C : (e + 1) * C], 3, s, lo + e * C, lo + (e + 1) * C, s + e == 0, s + e == 2)
            nc.scalar.activation(h[3][:, lo : lo + 2 * C], acc[:], RELU)

        def gather_scales(lo, hi):
            nc.vector.tensor_copy(gs[:, lo:hi], xs[:].indirect(offs_sb[:, lo // 16 : hi // 16]))

        for e in range(2):
            gather_words(0, e * C, (e + 1) * C)
        for half in range(2):
            gather_scales(half * 2 * C, (half + 1) * 2 * C)
        for e in range(2):
            gather_words(1, e * C, (e + 1) * C)
        hidden([(a, e * C, (e + 1) * C, 4 * e + a) for e in range(2) for a in range(3)])
        for s in range(PASSES):
            gather_words(s, 2 * C, 3 * C)
        hidden([(a, 2 * C, 3 * C, a) for a in range(3)])
        gather_words(0, 3 * C, S)
        gather_words(1, 3 * C, 3 * C + P)
        gather_words(1, 3 * C + P, S)
        hidden([(0, 3 * C, 3 * C + P, 3), (0, 3 * C + P, S, 7), (1, 3 * C, S, 4), (2, 3 * C, S, 5)])

        w2_bf = held("w2_bf", [P, N, 4], BF16)
        w2_codes = held("w2_codes", [P, N], U32)
        w2_scales = held("w2_scales", [P, N], U8)
        nc.vector.tensor_copy(w2_bf[:], w2_raw[:].rearrange("p j n -> p n j"))
        nc.vector.quantize_mx(
            out=w2_codes[:].bitcast(FP8X4), scales=w2_scales[:], in_=w2_bf[:].rearrange("p n j -> p (n j)")
        )

        ct = [held(f"ct{half}", [P, 2 * H], BF16) for half in range(2)]

        def rounded(b0, blocks):
            return ct[b0 // 2][:, b0 % 2 * H : (b0 % 2 + blocks) * H]

        def fetched(a, b0, blocks, gated, name):
            t0, width = b0 * P, blocks * P
            tiles = [held(f"{name}_{r}", [P, width], F32) for r in range(2)]
            for r in range(2):
                columns = h[a][:].indirect(pos_sb[r][:, t0 // 16 : (t0 + width) // 16])
                if gated:
                    nc.vector.tensor_tensor(tiles[r][:], columns, gate_sb[b0 // 2][:, r, b0 % 2 * P : b0 % 2 * P + width], MULT)
                else:
                    nc.scalar.activation(tiles[r][:], columns, COPY)
            return tiles

        def add_gated(a, b0, sums):
            blocks = sums.shape[1] // P
            tiles = fetched(a, b0, blocks, True, f"gated{a}_{b0}")
            for r in range(2):
                for b in range(blocks):
                    nc.tensor.matmul(
                        sums[:, b * P : (b + 1) * P],
                        lhsT=tiles[r][:, b * P : (b + 1) * P],
                        rhs=ident[:],
                        start=r + b == 0,
                        stop=r == 1 and b == blocks - 1,
                        is_transpose=True,
                    )

        def round_sums(b0, blocks, a0, sums):
            rows = sums.shape[1] // blocks // 4
            nc.scalar.copy(
                rounded(b0, blocks).rearrange("t (b u p e) -> t b u p e", u=2, p=P, e=2)[
                    :, :, :, 32 * a0 : 32 * a0 + rows, :
                ],
                sums.rearrange("t (b p u e) -> t b u p e", p=rows, u=2, e=2),
            )

        def combine(a, b0, blocks, n):
            sums = bank(n)[:, : blocks * P]
            add_gated(a, b0, sums)
            return sums

        def turn_plain(a, tiles, col, both):
            for r in range(2):
                at = (2 * r + a % 2) * P
                nc.tensor.transpose(both[:, at : at + P], tiles[r][:, col : col + P], ident[:])

        def scale_on_scalar(dst, src, factor):
            nc.scalar.activation(dst, src, COPY, scale=factor)

        def scale_on_vector(dst, src, factor):
            nc.vector.tensor_scalar(dst, src, factor, None, MULT)

        def weigh(b, both, scale):
            first = held(f"first{b}", [P, 2, P], F32)
            scale(
                first[:].rearrange("t u (p e) -> t u p e", e=2),
                both[:, : 2 * P].rearrange("t (p u e) -> t u p e", u=2, e=2),
                gate_col[0][:, b - 1 : b],
            )
            for u in range(2):
                nc.vector.scalar_tensor_tensor(
                    rounded(b, 1)[:, u * 2 * P : u * 2 * P + P].rearrange("t (p e) -> t p e", e=2),
                    both[:, 2 * P :].rearrange("t (p u e) -> t u p e", u=2, e=2)[:, u],
                    gate_col[1][:, b - 1 : b],
                    first[:, u, :].rearrange("t (p e) -> t p e", e=2),
                    MULT,
                    ADD,
                )

        res = held("res", [P, T], F32)

        def turn_back(b0, blocks, n):
            back = bank(n)
            width = blocks * P
            for b in range(blocks):
                words = rounded(b0 + b, 1).bitcast(F32)
                for u in range(2):
                    nc.tensor.transpose(
                        back[:, u * width + b * P : u * width + (b + 1) * P], words[:, u * P : (u + 1) * P], ident[:]
                    )
            return back[:, : 2 * width].rearrange("p (u t) -> p t u", u=2)

        c_bf = held("c_bf", [P, T * 4], BF16)

        def lay_out(b, n, copy):
            copy(c_bf[:, b * BANK : (b + 1) * BANK].bitcast(F32).rearrange("p (t u) -> p t u", u=2), turn_back(b, 1, n))

        def project(t0, width, n, copy_result):
            codes = held(f"c_codes{t0}", [P, width], U32)
            scales = held(f"c_scales{t0}", [P, width], U8)
            nc.vector.quantize_mx(out=codes[:].bitcast(FP8X4), scales=scales[:], in_=c_bf[:, 4 * t0 : 4 * (t0 + width)])
            proj = bank(n)
            nc.tensor.matmul_mx(
                out=proj[:, :width],
                lhsT=w2_codes[:].bitcast(FP8X4),
                lhsT_scale=w2_scales[:],
                rhs=codes[:].bitcast(FP8X4),
                rhs_scale=scales[:],
                start=True,
                stop=True,
            )
            copy_result(res[:, t0 : t0 + width], proj[:, :width])

        def store(t0, width):
            nc.sync.dma_start(out[:, t0 : t0 + width], res[:, t0 : t0 + width])

        hidden_late(0, 1)
        hidden_late(2 * C, 2)
        low = [bank(n) for n in (4, 5, 6, 3)]
        for a in range(2):
            add_gated(a, 0, low[0][:, a * P : (a + 1) * P])
        third = [combine(2, 0, 2, 0)]
        for a in range(2):
            turn_plain(a, fetched(a, 1, 1, False, f"plain{a}_1"), 0, low[1])
        third.append(combine(2, 2, 2, 7))
        plain = fetched(0, 2, 2, False, "plain0_2")
        for b in (2, 3):
            turn_plain(0, plain, (b - 2) * P, low[b])
        fourth = combine(3, 0, 2, 1)
        plain = fetched(1, 2, 2, False, "plain1_2")
        for b in (2, 3):
            turn_plain(1, plain, (b - 2) * P, low[b])
        round_sums(0, 1, 0, low[0][:, : 2 * P])
        last = [combine(3, 2, 1, 2), combine(3, 3, 1, 4)]
        round_sums(0, 2, 2, third[0])
        round_sums(0, 2, 3, fourth)
        first_pairs = turn_back(0, 1, 0)
        weigh(1, low[1], scale_on_scalar)
        weigh(2, low[2], scale_on_scalar)
        nc.vector.tensor_copy(c_bf[:, :BANK].bitcast(F32).rearrange("p (t u) -> p t u", u=2), first_pairs)
        round_sums(2, 2, 2, third[1])
        weigh(3, low[3], scale_on_scalar)
        round_sums(2, 1, 3, last[0])
        round_sums(3, 1, 3, last[1])
        lay_out(1, 1, nc.scalar.copy)
        project(0, 2 * P, 2, nc.scalar.copy)
        store(0, 2 * P)
        lay_out(2, 5, nc.vector.tensor_copy)
        project(2 * P, P, 6, nc.vector.tensor_copy)
        store(2 * P, P)
        lay_out(3, 7, nc.scalar.copy)
        project(3 * P, P, 3, nc.scalar.copy)
        store(3 * P, P)
